import numpy as np
import ml_dtypes


def mxq(x, axis, fmt="e4m3"):
    dtype, down = {"e4m3": (ml_dtypes.float8_e4m3fn, 7), "e5m2": (ml_dtypes.float8_e5m2, 14)}[fmt]
    v = np.moveaxis(np.asarray(x, np.float32).astype(ml_dtypes.bfloat16).astype(np.float64), axis, -1)
    blocks = v.reshape(v.shape[:-1] + (-1, 32))
    amax = np.abs(blocks).max(-1, keepdims=True)
    byte = np.maximum(np.where(amax > 0, np.frexp(amax)[1] - 1 + 127, 0) - down, 1)
    scale = np.exp2(byte - 127.0)
    codes = (blocks / scale).astype(np.float32).astype(dtype).astype(np.float64)
    return np.moveaxis((codes * scale).reshape(v.shape), -1, axis)


WIDE = False


def mx_kscale(k):
    if not WIDE:
        return np.ones(k)
    levels = np.array([10, -10, 5, -5, 0])
    if k % 512:
        return np.exp2(np.random.permutation(np.resize(levels, k // 32))).repeat(32)
    a = np.empty((k // 512, 16))
    for p in range(k // 512):
        a[p, :8] = np.random.permutation(np.resize(levels, 8))
        for g in range(8):
            far = levels[np.abs(levels - a[p, g]) >= 10]
            a[p, g + 8] = far[np.random.randint(len(far))]
    return np.exp2(a.ravel()).repeat(32)


def f64(x):
    return np.asarray(x).astype(np.float64)


def striped(idx):
    return np.tile(idx.reshape(-1, 16).T, (8, 1)).astype(np.uint16)


def unstriped(offs):
    return offs[:16].T.reshape(-1).astype(np.int64)


def pack_weight(w):
    k, n = w.shape
    w = f64(np.asarray(w, np.float32).astype(ml_dtypes.bfloat16)).reshape(k // 32, 32, n)
    amax = np.abs(w).max(1)
    byte = np.clip(np.where(amax > 0, np.frexp(amax)[1] - 1 + 127 - 7, 1), 1, 254)
    scaled = (w * np.exp2(127.0 - byte)[:, None, :]).reshape(k, n).astype(np.float32)
    words = np.ascontiguousarray(scaled.reshape(k // 512, 128, 4, n).transpose(0, 1, 3, 2)).astype(ml_dtypes.float8_e4m3fn).view(np.uint8)
    return words, np.ascontiguousarray(byte.astype(np.uint8).reshape(k // 512, 16, n))


def unpack_weight(words, scales):
    g, p, n, _ = words.shape
    vals = np.ascontiguousarray(words).view(ml_dtypes.float8_e4m3fn).astype(np.float64) * np.repeat(np.exp2(scales.astype(np.float64) - 127.0), 8, axis=1)[..., None]
    return vals.transpose(0, 1, 3, 2).reshape(g * 512, n)


K, T, S, N, V, W = 512, 4096, 1024, 256, 512, 1024


def setup_inputs():
    n = np.random.standard_normal
    s = mx_kscale(K)[:, None]
    c = mx_kscale(S)
    packed_xT = pack_weight(n((K, T)) * s)
    packed_eT = pack_weight(n((K, W)) / np.sqrt(K) / s)
    return {
        "x_words": packed_xT[0],
        "x_scales": packed_xT[1],
        "e_words": packed_eT[0],
        "e_scales": packed_eT[1],
        "mask": (np.random.uniform(0.3, 1.0, (S, 1)) * c[:, None]).astype(np.float32),
        "wv": (n((K, N)) / np.sqrt(K) / s).astype(np.float32),
        "inv": (np.random.uniform(0.6, 1.4, (S, 1)) / c[:, None]).astype(np.float32),
        "offs": striped(np.random.permutation(T)[:S]),
        "slot": striped(np.random.permutation(W)[:V]),
    }


def reference(x_words, x_scales, e_words, e_scales, mask, wv, inv, offs, slot):
    xq = unpack_weight(x_words, x_scales)[:, unstriped(offs)]
    wvq = mxq(f64(wv), 0, "e4m3")
    h = f64(inv) * (xq.T @ wvq)
    e_slot = unpack_weight(e_words, e_scales)[:, unstriped(slot)]
    y = xq.T @ e_slot
    ex = np.exp(y - y.max(axis=1, keepdims=True))
    p = ex / ex.sum(axis=1, keepdims=True)
    a = f64(mask) * p
    return mxq(h, 0, "e4m3").T @ mxq(a, 0, "e4m3")

@@ -1,0 +1,264 @@
+from contextlib import ExitStack
+
+import concourse.mybir as mybir
+from concourse.masks import make_identity
+
+K, T, S, N, V, W = 512, 4096, 1024, 256, 512, 1024
+FLOPS = 2 * S * K * N + 2 * S * K * V + 2 * S * N * V
+
+F32 = mybir.dt.float32
+BF16 = mybir.dt.bfloat16
+I32 = mybir.dt.int32
+U32 = mybir.dt.uint32
+U16 = mybir.dt.uint16
+U8 = mybir.dt.uint8
+FP8X4 = mybir.dt.float8_e4m3fn_x4
+ACT = mybir.ActivationFunctionType
+ALU = mybir.AluOpType
+
+P = 128
+PACK = 4
+PASS = P * PACK
+GROUPS = S // PASS
+RUN = 8
+HALF = V // 2
+FREE_ROWS = P - 16
+TOKEN_ROW = P - 2 * PACK
+
+
+def tile_picked_yslot_soft_p_kernel(
+    tc, x_words, x_scales, e_words, e_scales, mask, wv, inv, offs, slot, out
+):
+    nc = tc.nc
+    with ExitStack() as ctx:
+        keep = ctx.enter_context(tc.tile_pool(name="keep", bufs=1))
+        psum = ctx.enter_context(tc.psum_pool(name="psum", bufs=1))
+
+        def sb(name, shape, dtype):
+            return keep.tile(shape, dtype, name=name, align_bytes=64)
+
+        def bank(name, number, shape):
+            return psum.tile(shape, F32, name=name, tag="bank%d" % number)
+
+        offs_sb = keep.tile([P, S // 16], U16, name="offs_sb")
+        slot_sb = keep.tile([P, V // 16], U16, name="slot_sb")
+        xw_all = sb("xw_all", [P, T], I32)
+        ew_all = sb("ew_all", [P, W], I32)
+        xs_all = sb("xs_all", [P, T], U8)
+        es_all = sb("es_all", [P, W], U8)
+        wv_raw = sb("wv_raw", [P, PACK, N], F32)
+        token_rows = sb("token_rows", [P, GROUPS, P], F32)
+        token_cols = sb("token_cols", [P, GROUPS, 2 * PACK], F32)
+        identity = sb("identity", [P, P], F32)
+
+        scales = sb("scales", [P, S + V], U8)
+        nc.vector.memset(xs_all[0:FREE_ROWS, :].bitcast(I32), 0)
+        nc.gpsimd.memset(es_all[0:FREE_ROWS, :].bitcast(I32), 0)
+        nc.gpsimd.memset(scales[:].bitcast(I32), 0)
+
+        nc.sync.dma_start(offs_sb[:], offs)
+        nc.sync.dma_start(xs_all[FREE_ROWS:P, :].bitcast(I32), x_scales[0].bitcast(I32))
+        nc.sync.dma_start(slot_sb[:], slot)
+        nc.sync.dma_start(es_all[FREE_ROWS:P, :].bitcast(I32), e_scales[0].bitcast(I32))
+        nc.sync.dma_start(ew_all[:], e_words[0].rearrange("p n t -> p (n t)").bitcast(I32))
+        nc.sync.dma_start(xw_all[:], x_words[0].rearrange("p n t -> p (n t)").bitcast(I32))
+        nc.sync.dma_start(wv_raw[:], wv.rearrange("(p j) m -> p j m", j=PACK))
+        for row, src in ((TOKEN_ROW, mask), (TOKEN_ROW + PACK, inv)):
+            nc.scalar.dma_start(
+                token_rows[row : row + PACK].rearrange("j g (b i) -> j (g b) i", i=RUN),
+                src.rearrange("(b j i) o -> j b (i o)", j=PACK, i=RUN),
+            )
+        nc.gpsimd.memset(token_rows[0:TOKEN_ROW], 0.0)
+        make_identity(nc, identity[:])
+        turned = bank("turned", 6, [P, GROUPS, P])
+        for g in range(GROUPS):
+            nc.tensor.transpose(turned[:, g, :], token_rows[:, g, :], identity[:])
+        nc.scalar.activation(token_cols[:], turned[:, :, TOKEN_ROW:P], ACT.Copy)
+
+        xs_list = sb("xs_list", [P, S], U8)
+        dealt = sb("dealt", [P, S + V], U8)
+        xw = [sb("xw%d" % g, [P, PASS], U32) for g in range(GROUPS)]
+        ew = sb("ew", [P, V], U32)
+        es_list = sb("es_list", [P, V], U8)
+
+        def offs_of(g):
+            return offs_sb[:, g * PASS // 16 : (g + 1) * PASS // 16]
+
+        nc.vector.tensor_copy(xs_list[:], xs_all[:].indirect(offs_sb[:]))
+        nc.vector.tensor_copy(es_list[:], es_all[:].indirect(slot_sb[:]))
+        nc.vector.tensor_copy(
+            dealt[:, 0:S].bitcast(I32).rearrange("p (g j b w) -> p g j b w", g=GROUPS, j=PACK, w=RUN // 4),
+            xs_list[:].bitcast(I32).rearrange("p (g b j w) -> p g j b w", g=GROUPS, j=PACK, w=RUN // 4),
+        )
+        nc.vector.tensor_copy(dealt[:, S : S + V].bitcast(I32), es_list[:].bitcast(I32))
+        for q in range(4):
+            nc.scalar.dma_start(
+                scales[32 * q : 32 * q + 4, :].bitcast(I32),
+                dealt[FREE_ROWS + 4 * q : FREE_ROWS + 4 * q + 4, :].bitcast(I32),
+            )
+        nc.vector.tensor_copy(ew[:], ew_all[:].bitcast(U32).indirect(slot_sb[:]))
+        for g in range(GROUPS):
+            nc.vector.tensor_copy(
+                xw[g][:].rearrange("p (j b i) -> p b j i", j=PACK, i=RUN),
+                xw_all[:].bitcast(U32).indirect(offs_of(g)),
+            )
+
+        wv_bf = sb("wv_bf", [P, N, PACK], BF16)
+        wv_w = sb("wv_w", [P, N], U32)
+        wv_s = sb("wv_s", [P, N], U8)
+
+        def prepare_wv():
+            nc.scalar.copy(
+                wv_bf[:].rearrange("p (c i) j -> p c j i", i=4), wv_raw[:].rearrange("p j (c i) -> p c j i", i=4)
+            )
+            nc.vector.quantize_mx(wv_w[:].bitcast(FP8X4), wv_s[:], wv_bf[:].rearrange("p m j -> p (m j)"))
+
+        tiles = GROUPS * PACK
+        neg_max = [sb("neg_max%d" % s, [P, 1], F32) for s in range(tiles)]
+        batches = ((0, 1), (2, 3), (4, 5), (6,), (7,))
+        total, recip, factor = {}, {}, {}
+        for batch in batches:
+            for name, store_in in (("total", total), ("recip", recip), ("factor", factor)):
+                store_in[batch] = sb("%s%d" % (name, batch[0]), [P, len(batch)], F32)
+
+        def column(tiles_by_batch, s):
+            batch = [b for b in batches if s in b][0]
+            return tiles_by_batch[batch][:, s - batch[0] : s - batch[0] + 1]
+
+        ex = [sb("ex%d" % s, [P, V], F32) for s in range(tiles)]
+        a_rows = [sb("a_rows%d" % g, [P, 2, PACK, HALF], BF16) for g in range(GROUPS)]
+        h_woven = [sb("h_woven%d" % g, [P, N, PACK], BF16) for g in range(GROUPS)]
+        a_w = [[sb("a_w%d_%d" % (g, c), [P, HALF], U32) for c in range(2)] for g in range(GROUPS)]
+        a_s = [[sb("a_s%d_%d" % (g, c), [P, HALF], U8) for c in range(2)] for g in range(GROUPS)]
+        h_w = [sb("h_w%d" % g, [P, N], U32) for g in range(GROUPS)]
+        h_s = [sb("h_s%d" % g, [P, N], U8) for g in range(GROUPS)]
+
+        def token_operand(s):
+            g, j = divmod(s, PACK)
+            cols = slice(j * P, (j + 1) * P)
+            return dict(lhsT=xw[g][:, cols].bitcast(FP8X4), lhsT_scale=scales[:, s * P : (s + 1) * P])
+
+        def logits(s):
+            y = bank("y%d" % s, s % 4, [P, V])
+            nc.tensor.matmul_mx(
+                y[:], rhs=ew[:].bitcast(FP8X4), rhs_scale=scales[:, S : S + V], start=True, stop=True, **token_operand(s)
+            )
+            nc.vector.tensor_reduce(neg_max[s][:], y[:], mybir.AxisListType.X, ALU.max, negate=True)
+            nc.scalar.activation(
+                ex[s][:], y[:], ACT.Exp, bias=neg_max[s][:], accum_out=column(total, s)
+            )
+
+        def values(g, mh):
+            cols = slice(mh * P, (mh + 1) * P)
+            h = bank("h%d_%d" % (g, mh), 4 + mh, [P, PACK, P])
+            for j in range(PACK):
+                nc.tensor.matmul_mx(
+                    h[:, j, :], rhs=wv_w[:, cols].bitcast(FP8X4), rhs_scale=wv_s[:, cols], start=True, stop=True,
+                    **token_operand(PACK * g + j)
+                )
+            nc.vector.tensor_tensor(
+                h_woven[g][:, cols, :],
+                h[:].rearrange("p j m -> p m j"),
+                token_cols[:, g, PACK : 2 * PACK].unsqueeze(1).to_broadcast([P, P, PACK]),
+                ALU.mult,
+            )
+
+        def factors(u):
+            batch = batches[u]
+            g, j = divmod(batch[0], PACK)
+            nc.vector.reciprocal(recip[batch][:], total[batch][:])
+            nc.vector.tensor_tensor(factor[batch][:], recip[batch][:], token_cols[:, g, j : j + len(batch)], ALU.mult)
+
+        def weights(s, halves):
+            g, j = divmod(s, PACK)
+            nc.scalar.activation(
+                a_rows[g][:, halves, j, :],
+                ex[s][:].rearrange("p (c v) -> p c v", c=2)[:, halves, :],
+                ACT.Copy,
+                scale=column(factor, s),
+            )
+
+        def weave(name, rows, width):
+            woven = sb(name, [P, width, PACK], BF16)
+            nc.vector.tensor_copy(
+                woven[:].rearrange("p (c i) j -> p c j i", i=4), rows.rearrange("p j (c i) -> p c j i", i=4)
+            )
+            return woven[:].rearrange("p v j -> p (v j)")
+
+        def weave_a(g, c):
+            return weave("a_woven%d_%d" % (g, c), a_rows[g][:, c], HALF)
+
+        def quantize_a(g, c, woven):
+            nc.vector.quantize_mx(a_w[g][c][:].bitcast(FP8X4), a_s[g][c][:], woven)
+
+        def quantize_h(g):
+            nc.vector.quantize_mx(h_w[g][:].bitcast(FP8X4), h_s[g][:], h_woven[g][:].rearrange("p m j -> p (m j)"))
+
+        acc = {}
+
+        def update(g, c):
+            for mh in range(2):
+                if g == 0:
+                    acc[c, mh] = bank("acc%d_%d" % (c, mh), (6, 7, 0, 1)[2 * c + mh], [P, HALF])
+                cols = slice(mh * P, (mh + 1) * P)
+                nc.tensor.matmul_mx(
+                    acc[c, mh][:],
+                    lhsT=h_w[g][:, cols].bitcast(FP8X4),
+                    lhsT_scale=h_s[g][:, cols],
+                    rhs=a_w[g][c][:].bitcast(FP8X4),
+                    rhs_scale=a_s[g][c][:],
+                    start=(g == 0),
+                    stop=(g == GROUPS - 1),
+                )
+
+        def store(c, mh, copy, queue):
+            result = sb("result%d_%d" % (c, mh), [P, HALF], F32)
+            copy(result[:], acc[c, mh][:])
+            queue.dma_start(out[mh * P : (mh + 1) * P, c * HALF : (c + 1) * HALF], result[:])
+
+        both = slice(0, 2)
+        prepare_wv()
+        logits(0)
+        logits(1)
+        logits(2)
+        factors(0)
+        logits(3)
+        weights(0, both)
+        logits(4)
+        factors(1)
+        weights(1, both)
+        logits(5)
+        weights(2, both)
+        logits(6)
+        factors(2)
+        weights(3, both)
+        logits(7)
+        factors(3)
+        weights(4, both)
+        values(0, 0)
+        factors(4)
+        weights(5, both)
+        weights(6, both)
+        weights(7, slice(0, 1))
+        weights(7, slice(1, 2))
+        values(0, 1)
+        wa0 = weave_a(0, 0)
+        quantize_h(0)
+        wa1 = weave_a(0, 1)
+        quantize_a(0, 0, wa0)
+        values(1, 0)
+        quantize_a(0, 1, wa1)
+        update(0, 0)
+        update(0, 1)
+        values(1, 1)
+        wa0 = weave_a(1, 0)
+        quantize_h(1)
+        wa1 = weave_a(1, 1)
+        quantize_a(1, 0, wa0)
+        update(1, 0)
+        quantize_a(1, 1, wa1)
+        store(0, 0, nc.scalar.copy, nc.sync)
+        store(0, 1, nc.scalar.copy, nc.sync)
+        update(1, 1)
+        store(1, 0, nc.scalar.copy, nc.scalar)
+        store(1, 1, nc.vector.tensor_copy, nc.sync)

@@ -34,8 +34,8 @@ def tile_picked_yslot_soft_p_kernel(
         keep = ctx.enter_context(tc.tile_pool(name="keep", bufs=1))
         psum = ctx.enter_context(tc.psum_pool(name="psum", bufs=1))
 
-        def sb(name, shape, dtype):
-            return keep.tile(shape, dtype, name=name, align_bytes=64)
+        def sb(name, shape, dtype, tag=None):
+            return keep.tile(shape, dtype, name=name, tag=tag or name, align_bytes=64)
 
         def bank(name, number, shape):
             return psum.tile(shape, F32, name=name, tag="bank%d" % number)
@@ -53,8 +53,8 @@ def tile_picked_yslot_soft_p_kernel(
 
         scales = sb("scales", [P, S + V], U8)
         nc.vector.memset(xs_all[0:FREE_ROWS, :].bitcast(I32), 0)
-        nc.gpsimd.memset(es_all[0:FREE_ROWS, :].bitcast(I32), 0)
-        nc.gpsimd.memset(scales[:].bitcast(I32), 0)
+        nc.vector.memset(es_all[0:FREE_ROWS, :].bitcast(I32), 0)
+        nc.vector.memset(scales[:].bitcast(I32), 0)
 
         nc.sync.dma_start(offs_sb[:], offs)
         nc.sync.dma_start(xs_all[FREE_ROWS:P, :].bitcast(I32), x_scales[0].bitcast(I32))
@@ -68,7 +68,7 @@ def tile_picked_yslot_soft_p_kernel(
                 token_rows[row : row + PACK].rearrange("j g (b i) -> j (g b) i", i=RUN),
                 src.rearrange("(b j i) o -> j b (i o)", j=PACK, i=RUN),
             )
-        nc.gpsimd.memset(token_rows[0:TOKEN_ROW], 0.0)
+        nc.vector.memset(token_rows[0:TOKEN_ROW], 0.0)
         make_identity(nc, identity[:])
         turned = bank("turned", 6, [P, GROUPS, P])
         for g in range(GROUPS):
@@ -77,7 +77,7 @@ def tile_picked_yslot_soft_p_kernel(
 
         xs_list = sb("xs_list", [P, S], U8)
         dealt = sb("dealt", [P, S + V], U8)
-        xw = [sb("xw%d" % g, [P, PASS], U32) for g in range(GROUPS)]
+        xw = {}
         ew = sb("ew", [P, V], U32)
         es_list = sb("es_list", [P, V], U8)
 
@@ -92,12 +92,16 @@ def tile_picked_yslot_soft_p_kernel(
         )
         nc.vector.tensor_copy(dealt[:, S : S + V].bitcast(I32), es_list[:].bitcast(I32))
         for q in range(4):
-            nc.scalar.dma_start(
+            nc.sync.dma_start(
                 scales[32 * q : 32 * q + 4, :].bitcast(I32),
                 dealt[FREE_ROWS + 4 * q : FREE_ROWS + 4 * q + 4, :].bitcast(I32),
             )
-        nc.vector.tensor_copy(ew[:], ew_all[:].bitcast(U32).indirect(slot_sb[:]))
-        for g in range(GROUPS):
+
+        def gather_slots():
+            nc.vector.tensor_copy(ew[:], ew_all[:].bitcast(U32).indirect(slot_sb[:]))
+
+        def gather_tokens(g, tag):
+            xw[g] = sb("xw%d" % g, [P, PASS], U32, tag)
             nc.vector.tensor_copy(
                 xw[g][:].rearrange("p (j b i) -> p b j i", j=PACK, i=RUN),
                 xw_all[:].bitcast(U32).indirect(offs_of(g)),
@@ -115,7 +119,7 @@ def tile_picked_yslot_soft_p_kernel(
 
         tiles = GROUPS * PACK
         neg_max = [sb("neg_max%d" % s, [P, 1], F32) for s in range(tiles)]
-        batches = ((0, 1), (2, 3), (4, 5), (6,), (7,))
+        batches = ((0, 1, 2, 3), (4, 5, 6, 7))
         total, recip, factor = {}, {}, {}
         for batch in batches:
             for name, store_in in (("total", total), ("recip", recip), ("factor", factor)):
@@ -128,8 +132,9 @@ def tile_picked_yslot_soft_p_kernel(
         ex = [sb("ex%d" % s, [P, V], F32) for s in range(tiles)]
         a_rows = [sb("a_rows%d" % g, [P, 2, PACK, HALF], BF16) for g in range(GROUPS)]
         h_woven = [sb("h_woven%d" % g, [P, N, PACK], BF16) for g in range(GROUPS)]
-        a_w = [[sb("a_w%d_%d" % (g, c), [P, HALF], U32) for c in range(2)] for g in range(GROUPS)]
-        a_s = [[sb("a_s%d_%d" % (g, c), [P, HALF], U8) for c in range(2)] for g in range(GROUPS)]
+        a_w = [sb("a_w%d" % g, [P, V], U32) for g in range(GROUPS)]
+        a_s = [sb("a_s%d" % g, [P, V], U8) for g in range(GROUPS)]
+        a_woven = [sb("a_woven%d" % g, [P, V, PACK], BF16) for g in range(GROUPS)]
         h_w = [sb("h_w%d" % g, [P, N], U32) for g in range(GROUPS)]
         h_s = [sb("h_s%d" % g, [P, N], U8) for g in range(GROUPS)]
 
@@ -148,19 +153,30 @@ def tile_picked_yslot_soft_p_kernel(
                 ex[s][:], y[:], ACT.Exp, bias=neg_max[s][:], accum_out=column(total, s)
             )
 
-        def values(g, mh):
-            cols = slice(mh * P, (mh + 1) * P)
-            h = bank("h%d_%d" % (g, mh), 4 + mh, [P, PACK, P])
-            for j in range(PACK):
+        h_rows = [sb("h_rows%d" % g, [P, PACK, N], BF16) for g in range(GROUPS)]
+
+        def values(g, u):
+            h = bank("h%d_%d" % (g, u), 4 + u, [P, 2, N])
+            for e in range(2):
                 nc.tensor.matmul_mx(
-                    h[:, j, :], rhs=wv_w[:, cols].bitcast(FP8X4), rhs_scale=wv_s[:, cols], start=True, stop=True,
-                    **token_operand(PACK * g + j)
+                    h[:, e, :], rhs=wv_w[:].bitcast(FP8X4), rhs_scale=wv_s[:], start=True, stop=True,
+                    **token_operand(PACK * g + 2 * u + e)
                 )
-            nc.vector.tensor_tensor(
-                h_woven[g][:, cols, :],
-                h[:].rearrange("p j m -> p m j"),
-                token_cols[:, g, PACK : 2 * PACK].unsqueeze(1).to_broadcast([P, P, PACK]),
-                ALU.mult,
+            for e in range(2):
+                j = 2 * u + e
+                nc.scalar.activation(
+                    h_rows[g][:, j, :], h[:, e, :], ACT.Copy, scale=token_cols[:, g, PACK + j : PACK + j + 1]
+                )
+
+        def weave_h(g):
+            nc.vector.tensor_copy(
+                h_woven[g][:].rearrange("p (c i) j -> p c j i", i=4), h_rows[g][:].rearrange("p j (c i) -> p c j i", i=4)
+            )
+
+        def weights_on_vector(s):
+            g, j = divmod(s, PACK)
+            nc.vector.tensor_scalar(
+                a_rows[g][:, :, j, :], ex[s][:].rearrange("p (c v) -> p c v", c=2), column(factor, s), None, ALU.mult
             )
 
         def factors(u):
@@ -178,18 +194,16 @@ def tile_picked_yslot_soft_p_kernel(
                 scale=column(factor, s),
             )
 
-        def weave(name, rows, width):
-            woven = sb(name, [P, width, PACK], BF16)
-            nc.vector.tensor_copy(
-                woven[:].rearrange("p (c i) j -> p c j i", i=4), rows.rearrange("p j (c i) -> p c j i", i=4)
-            )
-            return woven[:].rearrange("p v j -> p (v j)")
-
         def weave_a(g, c):
-            return weave("a_woven%d_%d" % (g, c), a_rows[g][:, c], HALF)
+            nc.vector.tensor_copy(
+                a_woven[g][:, c * HALF : (c + 1) * HALF, :].rearrange("p (c i) j -> p c j i", i=4),
+                a_rows[g][:, c].rearrange("p j (c i) -> p c j i", i=4),
+            )
 
-        def quantize_a(g, c, woven):
-            nc.vector.quantize_mx(a_w[g][c][:].bitcast(FP8X4), a_s[g][c][:], woven)
+        def quantize_a(g, cols):
+            nc.vector.quantize_mx(
+                a_w[g][:, cols].bitcast(FP8X4), a_s[g][:, cols], a_woven[g][:, cols, :].rearrange("p v j -> p (v j)")
+            )
 
         def quantize_h(g):
             nc.vector.quantize_mx(h_w[g][:].bitcast(FP8X4), h_s[g][:], h_woven[g][:].rearrange("p m j -> p (m j)"))
@@ -205,8 +219,8 @@ def tile_picked_yslot_soft_p_kernel(
                     acc[c, mh][:],
                     lhsT=h_w[g][:, cols].bitcast(FP8X4),
                     lhsT_scale=h_s[g][:, cols],
-                    rhs=a_w[g][c][:].bitcast(FP8X4),
-                    rhs_scale=a_s[g][c][:],
+                    rhs=a_w[g][:, c * HALF : (c + 1) * HALF].bitcast(FP8X4),
+                    rhs_scale=a_s[g][:, c * HALF : (c + 1) * HALF],
                     start=(g == 0),
                     stop=(g == GROUPS - 1),
                 )
@@ -216,47 +230,40 @@ def tile_picked_yslot_soft_p_kernel(
             copy(result[:], acc[c, mh][:])
             queue.dma_start(out[mh * P : (mh + 1) * P, c * HALF : (c + 1) * HALF], result[:])
 
-        both = slice(0, 2)
-        prepare_wv()
+        gather_slots()
+        gather_tokens(0, None)
         logits(0)
+        gather_tokens(1, None)
         logits(1)
-        logits(2)
+        prepare_wv()
+        for s in range(2, tiles):
+            logits(s)
         factors(0)
-        logits(3)
-        weights(0, both)
-        logits(4)
+        for g in range(GROUPS):
+            values(g, 0)
+            values(g, 1)
+        weights_on_vector(0)
+        weights_on_vector(1)
         factors(1)
-        weights(1, both)
-        logits(5)
-        weights(2, both)
-        logits(6)
-        factors(2)
-        weights(3, both)
-        logits(7)
-        factors(3)
-        weights(4, both)
-        values(0, 0)
-        factors(4)
-        weights(5, both)
-        weights(6, both)
-        weights(7, slice(0, 1))
-        weights(7, slice(1, 2))
-        values(0, 1)
-        wa0 = weave_a(0, 0)
+        for c in range(2):
+            for s in range(PACK, tiles):
+                weights(s, slice(c, c + 1))
+        weights_on_vector(2)
+        weights_on_vector(3)
+        weave_h(0)
+        weave_a(0, 0)
         quantize_h(0)
-        wa1 = weave_a(0, 1)
-        quantize_a(0, 0, wa0)
-        values(1, 0)
-        quantize_a(0, 1, wa1)
+        weave_a(0, 1)
+        weave_h(1)
+        quantize_a(0, slice(0, V))
         update(0, 0)
         update(0, 1)
-        values(1, 1)
-        wa0 = weave_a(1, 0)
+        weave_a(1, 0)
         quantize_h(1)
-        wa1 = weave_a(1, 1)
-        quantize_a(1, 0, wa0)
+        weave_a(1, 1)
+        quantize_a(1, slice(0, HALF))
         update(1, 0)
-        quantize_a(1, 1, wa1)
+        quantize_a(1, slice(HALF, V))
         store(0, 0, nc.scalar.copy, nc.sync)
         store(0, 1, nc.scalar.copy, nc.sync)
         update(1, 1)

@@ -23,7 +23,7 @@ GROUPS = S // PASS
 RUN = 8
 HALF = V // 2
 FREE_ROWS = P - 16
-TOKEN_ROW = P - 2 * PACK
+TOKEN_ROWS = 2 * GROUPS
 
 
 def tile_picked_yslot_soft_p_kernel(
@@ -47,8 +47,9 @@ def tile_picked_yslot_soft_p_kernel(
         xs_all = sb("xs_all", [P, T], U8)
         es_all = sb("es_all", [P, W], U8)
         wv_raw = sb("wv_raw", [P, PACK, N], F32)
-        token_rows = sb("token_rows", [P, GROUPS, P], F32)
-        token_cols = sb("token_cols", [P, GROUPS, 2 * PACK], F32)
+        token_list = sb("token_list", [TOKEN_ROWS, PASS], F32)
+        token_rows = sb("token_rows", [P, PACK, P], F32)
+        token_cols = sb("token_cols", [P, TOKEN_ROWS, PACK], F32)
         identity = sb("identity", [P, P], F32)
 
         scales = sb("scales", [P, S + V], U8)
@@ -63,17 +64,19 @@ def tile_picked_yslot_soft_p_kernel(
         nc.sync.dma_start(ew_all[:], e_words[0].rearrange("p n t -> p (n t)").bitcast(I32))
         nc.sync.dma_start(xw_all[:], x_words[0].rearrange("p n t -> p (n t)").bitcast(I32))
         nc.sync.dma_start(wv_raw[:], wv.rearrange("(p j) m -> p j m", j=PACK))
-        for row, src in ((TOKEN_ROW, mask), (TOKEN_ROW + PACK, inv)):
-            nc.scalar.dma_start(
-                token_rows[row : row + PACK].rearrange("j g (b i) -> j (g b) i", i=RUN),
-                src.rearrange("(b j i) o -> j b (i o)", j=PACK, i=RUN),
-            )
-        nc.vector.memset(token_rows[0:TOKEN_ROW], 0.0)
+        for row, src in ((0, mask), (GROUPS, inv)):
+            nc.scalar.dma_start(token_list[row : row + GROUPS, :], src.rearrange("(g t) o -> g (t o)", g=GROUPS))
+        nc.vector.memset(token_rows[:], 0.0)
         make_identity(nc, identity[:])
-        turned = bank("turned", 6, [P, GROUPS, P])
-        for g in range(GROUPS):
-            nc.tensor.transpose(turned[:, g, :], token_rows[:, g, :], identity[:])
-        nc.scalar.activation(token_cols[:], turned[:, :, TOKEN_ROW:P], ACT.Copy)
+        nc.scalar.activation(
+            token_rows[0:TOKEN_ROWS].rearrange("r j (b i) -> r j b i", i=RUN),
+            token_list[:].rearrange("r (b j i) -> r j b i", j=PACK, i=RUN),
+            ACT.Copy,
+        )
+        turned = bank("turned", 6, [P, PACK, P])
+        for j in range(PACK):
+            nc.tensor.transpose(turned[:, j, :], token_rows[:, j, :], identity[:])
+        nc.scalar.activation(token_cols[:], turned[:, :, 0:TOKEN_ROWS].rearrange("p j r -> p r j"), ACT.Copy)
 
         xs_list = sb("xs_list", [P, S], U8)
         dealt = sb("dealt", [P, S + V], U8)
@@ -165,7 +168,7 @@ def tile_picked_yslot_soft_p_kernel(
             for e in range(2):
                 j = 2 * u + e
                 nc.scalar.activation(
-                    h_rows[g][:, j, :], h[:, e, :], ACT.Copy, scale=token_cols[:, g, PACK + j : PACK + j + 1]
+                    h_rows[g][:, j, :], h[:, e, :], ACT.Copy, scale=token_cols[:, GROUPS + g, j : j + 1]
                 )
 
         def weave_h(g):

@@ -22,6 +22,7 @@ PASS = P * PACK
 GROUPS = S // PASS
 RUN = 8
 HALF = V // 2
+CHUNKS = ((0, 256), (256, 384), (384, 512))
 FREE_ROWS = P - 16
 TOKEN_ROWS = 2 * GROUPS
 
@@ -66,7 +67,7 @@ def tile_picked_yslot_soft_p_kernel(
         nc.sync.dma_start(wv_raw[:], wv.rearrange("(p j) m -> p j m", j=PACK))
         for row, src in ((0, mask), (GROUPS, inv)):
             nc.scalar.dma_start(token_list[row : row + GROUPS, :], src.rearrange("(g t) o -> g (t o)", g=GROUPS))
-        nc.vector.memset(token_rows[:], 0.0)
+        nc.gpsimd.memset(token_rows[:], 0.0)
         make_identity(nc, identity[:])
         nc.scalar.activation(
             token_rows[0:TOKEN_ROWS].rearrange("r j (b i) -> r j b i", i=RUN),
@@ -122,10 +123,10 @@ def tile_picked_yslot_soft_p_kernel(
 
         tiles = GROUPS * PACK
         neg_max = [sb("neg_max%d" % s, [P, 1], F32) for s in range(tiles)]
-        batches = ((0, 1, 2, 3), (4, 5, 6, 7))
+        batches = ((0, 1), (2, 3), (4, 5, 6, 7))
         total, recip, factor = {}, {}, {}
         for batch in batches:
-            for name, store_in in (("total", total), ("recip", recip), ("factor", factor)):
+            for name, store_in in (("total", total), ("recip", recip), ("factor", factor))[: 2 + batch[0] // PACK]:
                 store_in[batch] = sb("%s%d" % (name, batch[0]), [P, len(batch)], F32)
 
         def column(tiles_by_batch, s):
@@ -176,16 +177,23 @@ def tile_picked_yslot_soft_p_kernel(
                 h_woven[g][:].rearrange("p (c i) j -> p c j i", i=4), h_rows[g][:].rearrange("p j (c i) -> p c j i", i=4)
             )
 
-        def weights_on_vector(s):
+        def weights_on(engine, s):
             g, j = divmod(s, PACK)
-            nc.vector.tensor_scalar(
-                a_rows[g][:, :, j, :], ex[s][:].rearrange("p (c v) -> p c v", c=2), column(factor, s), None, ALU.mult
+            engine.tensor_scalar(
+                a_rows[g][:, :, j, :],
+                ex[s][:].rearrange("p (c v) -> p c v", c=2),
+                column(recip, s),
+                token_cols[:, g, j : j + 1],
+                ALU.mult,
+                ALU.mult,
             )
+
+        def reciprocals(u):
+            nc.vector.reciprocal(recip[batches[u]][:], total[batches[u]][:])
 
         def factors(u):
             batch = batches[u]
             g, j = divmod(batch[0], PACK)
-            nc.vector.reciprocal(recip[batch][:], total[batch][:])
             nc.vector.tensor_tensor(factor[batch][:], recip[batch][:], token_cols[:, g, j : j + len(batch)], ALU.mult)
 
         def weights(s, halves):
@@ -197,10 +205,11 @@ def tile_picked_yslot_soft_p_kernel(
                 scale=column(factor, s),
             )
 
-        def weave_a(g, c):
+        def weave_a(g, lo, hi):
+            c, first = divmod(lo, HALF)
             nc.vector.tensor_copy(
-                a_woven[g][:, c * HALF : (c + 1) * HALF, :].rearrange("p (c i) j -> p c j i", i=4),
-                a_rows[g][:, c].rearrange("p j (c i) -> p c j i", i=4),
+                a_woven[g][:, lo:hi, :].rearrange("p (c i) j -> p c j i", i=4),
+                a_rows[g][:, c, :, first : first + hi - lo].rearrange("p j (c i) -> p c j i", i=4),
             )
 
         def quantize_a(g, cols):
@@ -214,24 +223,27 @@ def tile_picked_yslot_soft_p_kernel(
         acc = {}
 
         def update(g, c):
+            lo, hi = CHUNKS[c]
             for mh in range(2):
                 if g == 0:
-                    acc[c, mh] = bank("acc%d_%d" % (c, mh), (6, 7, 0, 1)[2 * c + mh], [P, HALF])
+                    acc[c, mh] = bank("acc%d_%d" % (c, mh), (6, 7, 0, 1, 2, 3)[2 * c + mh], [P, hi - lo])
                 cols = slice(mh * P, (mh + 1) * P)
                 nc.tensor.matmul_mx(
                     acc[c, mh][:],
                     lhsT=h_w[g][:, cols].bitcast(FP8X4),
                     lhsT_scale=h_s[g][:, cols],
-                    rhs=a_w[g][:, c * HALF : (c + 1) * HALF].bitcast(FP8X4),
-                    rhs_scale=a_s[g][:, c * HALF : (c + 1) * HALF],
+                    rhs=a_w[g][:, lo:hi].bitcast(FP8X4),
+                    rhs_scale=a_s[g][:, lo:hi],
                     start=(g == 0),
                     stop=(g == GROUPS - 1),
                 )
 
-        def store(c, mh, copy, queue):
-            result = sb("result%d_%d" % (c, mh), [P, HALF], F32)
-            copy(result[:], acc[c, mh][:])
-            queue.dma_start(out[mh * P : (mh + 1) * P, c * HALF : (c + 1) * HALF], result[:])
+        def store(c, copies, queue):
+            lo, hi = CHUNKS[c]
+            result = sb("result%d" % c, [P, 2, hi - lo], F32)
+            for mh in range(2):
+                copies[mh](result[:, mh, :], acc[c, mh][:])
+            queue.dma_start(out[:, lo:hi].rearrange("(h p) v -> p h v", p=P), result[:])
 
         gather_slots()
         gather_tokens(0, None)
@@ -239,36 +251,41 @@ def tile_picked_yslot_soft_p_kernel(
         gather_tokens(1, None)
         logits(1)
         prepare_wv()
-        for s in range(2, tiles):
+        logits(2)
+        reciprocals(0)
+        weights_on(nc.gpsimd, 0)
+        weights_on(nc.gpsimd, 1)
+        for s in range(3, tiles):
             logits(s)
-        factors(0)
+        reciprocals(1)
         for g in range(GROUPS):
             values(g, 0)
             values(g, 1)
-        weights_on_vector(0)
-        weights_on_vector(1)
-        factors(1)
+        weights_on(nc.vector, 2)
+        reciprocals(2)
+        weights_on(nc.vector, 3)
+        factors(2)
         for c in range(2):
             for s in range(PACK, tiles):
                 weights(s, slice(c, c + 1))
-        weights_on_vector(2)
-        weights_on_vector(3)
         weave_h(0)
-        weave_a(0, 0)
+        weave_a(0, 0, HALF)
         quantize_h(0)
-        weave_a(0, 1)
-        weave_h(1)
+        weave_a(0, HALF, V)
         quantize_a(0, slice(0, V))
-        update(0, 0)
-        update(0, 1)
-        weave_a(1, 0)
+        weave_h(1)
+        for c in range(len(CHUNKS)):
+            update(0, c)
+        weave_a(1, *CHUNKS[0])
         quantize_h(1)
-        weave_a(1, 1)
-        quantize_a(1, slice(0, HALF))
+        weave_a(1, *CHUNKS[1])
+        quantize_a(1, slice(*CHUNKS[0]))
         update(1, 0)
-        quantize_a(1, slice(HALF, V))
-        store(0, 0, nc.scalar.copy, nc.sync)
-        store(0, 1, nc.scalar.copy, nc.sync)
+        weave_a(1, *CHUNKS[2])
+        quantize_a(1, slice(*CHUNKS[1]))
         update(1, 1)
-        store(1, 0, nc.scalar.copy, nc.scalar)
-        store(1, 1, nc.vector.tensor_copy, nc.sync)
+        quantize_a(1, slice(*CHUNKS[2]))
+        update(1, 2)
+        store(0, (nc.scalar.copy, nc.scalar.copy), nc.sync)
+        store(1, (nc.scalar.copy, nc.scalar.copy), nc.sync)
+        store(2, (nc.scalar.copy, nc.vector.tensor_copy), nc.sync)

@@ -96,7 +96,7 @@ def tile_picked_yslot_soft_p_kernel(
         )
         nc.vector.tensor_copy(dealt[:, S : S + V].bitcast(I32), es_list[:].bitcast(I32))
         for q in range(4):
-            nc.sync.dma_start(
+            nc.scalar.dma_start(
                 scales[32 * q : 32 * q + 4, :].bitcast(I32),
                 dealt[FREE_ROWS + 4 * q : FREE_ROWS + 4 * q + 4, :].bitcast(I32),
             )

@@ -25,6 +25,7 @@ HALF = V // 2
 CHUNKS = ((0, 256), (256, 384), (384, 512))
 FREE_ROWS = P - 16
 TOKEN_ROWS = 2 * GROUPS
+TILES = GROUPS * PACK
 
 
 def tile_picked_yslot_soft_p_kernel(
@@ -74,19 +75,16 @@ def tile_picked_yslot_soft_p_kernel(
             token_list[:].rearrange("r (b j i) -> r j b i", j=PACK, i=RUN),
             ACT.Copy,
         )
-        turned = bank("turned", 6, [P, PACK, P])
+        turned = bank("turned", 7, [P, PACK, P])
         for j in range(PACK):
             nc.tensor.transpose(turned[:, j, :], token_rows[:, j, :], identity[:])
         nc.scalar.activation(token_cols[:], turned[:, :, 0:TOKEN_ROWS].rearrange("p j r -> p r j"), ACT.Copy)
 
         xs_list = sb("xs_list", [P, S], U8)
-        dealt = sb("dealt", [P, S + V], U8)
-        xw = {}
-        ew = sb("ew", [P, V], U32)
         es_list = sb("es_list", [P, V], U8)
-
-        def offs_of(g):
-            return offs_sb[:, g * PASS // 16 : (g + 1) * PASS // 16]
+        dealt = sb("dealt", [P, S + V], U8)
+        xw = [sb("xw%d" % g, [P, PASS], U32) for g in range(GROUPS)]
+        ew = sb("ew", [P, V], U32)
 
         nc.vector.tensor_copy(xs_list[:], xs_all[:].indirect(offs_sb[:]))
         nc.vector.tensor_copy(es_list[:], es_all[:].indirect(slot_sb[:]))
@@ -96,7 +94,7 @@ def tile_picked_yslot_soft_p_kernel(
         )
         nc.vector.tensor_copy(dealt[:, S : S + V].bitcast(I32), es_list[:].bitcast(I32))
         for q in range(4):
-            nc.scalar.dma_start(
+            nc.sync.dma_start(
                 scales[32 * q : 32 * q + 4, :].bitcast(I32),
                 dealt[FREE_ROWS + 4 * q : FREE_ROWS + 4 * q + 4, :].bitcast(I32),
             )
@@ -104,129 +102,100 @@ def tile_picked_yslot_soft_p_kernel(
         def gather_slots():
             nc.vector.tensor_copy(ew[:], ew_all[:].bitcast(U32).indirect(slot_sb[:]))
 
-        def gather_tokens(g, tag):
-            xw[g] = sb("xw%d" % g, [P, PASS], U32, tag)
+        def gather_tokens(g):
             nc.vector.tensor_copy(
                 xw[g][:].rearrange("p (j b i) -> p b j i", j=PACK, i=RUN),
-                xw_all[:].bitcast(U32).indirect(offs_of(g)),
+                xw_all[:].bitcast(U32).indirect(offs_sb[:, g * PASS // 16 : (g + 1) * PASS // 16]),
             )
 
         wv_bf = sb("wv_bf", [P, N, PACK], BF16)
         wv_w = sb("wv_w", [P, N], U32)
         wv_s = sb("wv_s", [P, N], U8)
 
-        def prepare_wv():
-            nc.scalar.copy(
-                wv_bf[:].rearrange("p (c i) j -> p c j i", i=4), wv_raw[:].rearrange("p j (c i) -> p c j i", i=4)
-            )
-            nc.vector.quantize_mx(wv_w[:].bitcast(FP8X4), wv_s[:], wv_bf[:].rearrange("p m j -> p (m j)"))
+        def weave(copy, woven, rows):
+            copy(woven.rearrange("p (c i) j -> p c j i", i=4), rows.rearrange("p j (c i) -> p c j i", i=4))
 
-        tiles = GROUPS * PACK
-        neg_max = [sb("neg_max%d" % s, [P, 1], F32) for s in range(tiles)]
-        batches = ((0, 1), (2, 3), (4, 5, 6, 7))
-        total, recip, factor = {}, {}, {}
-        for batch in batches:
-            for name, store_in in (("total", total), ("recip", recip), ("factor", factor))[: 2 + batch[0] // PACK]:
-                store_in[batch] = sb("%s%d" % (name, batch[0]), [P, len(batch)], F32)
-
-        def column(tiles_by_batch, s):
-            batch = [b for b in batches if s in b][0]
-            return tiles_by_batch[batch][:, s - batch[0] : s - batch[0] + 1]
-
-        ex = [sb("ex%d" % s, [P, V], F32) for s in range(tiles)]
-        a_rows = [sb("a_rows%d" % g, [P, 2, PACK, HALF], BF16) for g in range(GROUPS)]
-        h_woven = [sb("h_woven%d" % g, [P, N, PACK], BF16) for g in range(GROUPS)]
-        a_w = [sb("a_w%d" % g, [P, V], U32) for g in range(GROUPS)]
-        a_s = [sb("a_s%d" % g, [P, V], U8) for g in range(GROUPS)]
-        a_woven = [sb("a_woven%d" % g, [P, V, PACK], BF16) for g in range(GROUPS)]
-        h_w = [sb("h_w%d" % g, [P, N], U32) for g in range(GROUPS)]
-        h_s = [sb("h_s%d" % g, [P, N], U8) for g in range(GROUPS)]
+        def quantize(words, scale_bytes, woven):
+            nc.vector.quantize_mx(words.bitcast(FP8X4), scale_bytes, woven.rearrange("p m j -> p (m j)"))
 
         def token_operand(s):
             g, j = divmod(s, PACK)
-            cols = slice(j * P, (j + 1) * P)
-            return dict(lhsT=xw[g][:, cols].bitcast(FP8X4), lhsT_scale=scales[:, s * P : (s + 1) * P])
+            return dict(
+                lhsT=xw[g][:, j * P : (j + 1) * P].bitcast(FP8X4), lhsT_scale=scales[:, s * P : (s + 1) * P]
+            )
 
-        def logits(s):
-            y = bank("y%d" % s, s % 4, [P, V])
+        def mask_of(s):
+            g, j = divmod(s, PACK)
+            return token_cols[:, g, j : j + 1]
+
+        BATCHES = ((0,), (1, 2), (3, 4, 5), (6, 7))
+        neg_max = [sb("neg_max%d" % s, [P, 1], F32) for s in range(TILES)]
+        total = [sb("total%d" % u, [P, len(batch)], F32) for u, batch in enumerate(BATCHES[:-1])]
+        total.append(sb("total3", [P, 2], F32, "h_woven1"))
+        recip = [sb("recip%d" % u, [P, len(batch)], F32) for u, batch in enumerate(BATCHES)]
+        factor = {s: sb("factor%d" % s, [P, 1], F32) for s in (5, 6, 7)}
+        ex = [sb("ex%d" % s, [P, V], F32) for s in range(TILES)]
+        a_pairs = sb("a_pairs", [P, 2, V, 2], BF16)
+        a_rows = sb("a_rows", [P, PACK, V], BF16)
+        h_woven = {}
+        h_w = [sb("h_w%d" % g, [P, N], U32) for g in range(GROUPS)]
+        h_s = [sb("h_s%d" % g, [P, N], U8) for g in range(GROUPS)]
+        a_w = [sb("a_w%d" % g, [P, V], U32) for g in range(GROUPS)]
+        a_s = [sb("a_s%d" % g, [P, V], U8) for g in range(GROUPS)]
+        a_half = {}
+        a_chunk = {}
+
+        def column(tiles, s, n=1):
+            u = [s in batch for batch in BATCHES].index(True)
+            first = s - BATCHES[u][0]
+            return tiles[u][:, first : first + n]
+
+        def logits(s, number):
+            y = bank("y%d" % s, number, [P, V])
             nc.tensor.matmul_mx(
                 y[:], rhs=ew[:].bitcast(FP8X4), rhs_scale=scales[:, S : S + V], start=True, stop=True, **token_operand(s)
             )
             nc.vector.tensor_reduce(neg_max[s][:], y[:], mybir.AxisListType.X, ALU.max, negate=True)
-            nc.scalar.activation(
-                ex[s][:], y[:], ACT.Exp, bias=neg_max[s][:], accum_out=column(total, s)
-            )
+            nc.scalar.activation(ex[s][:], y[:], ACT.Exp, bias=neg_max[s][:], accum_out=column(total, s))
 
-        h_rows = [sb("h_rows%d" % g, [P, PACK, N], BF16) for g in range(GROUPS)]
-
-        def values(g, u):
-            h = bank("h%d_%d" % (g, u), 4 + u, [P, 2, N])
-            for e in range(2):
+        def values(g, u, number):
+            h = bank("h%d_%d" % (g, u), number, [P, PACK, P])
+            cols = slice(u * P, (u + 1) * P)
+            for j in range(PACK):
                 nc.tensor.matmul_mx(
-                    h[:, e, :], rhs=wv_w[:].bitcast(FP8X4), rhs_scale=wv_s[:], start=True, stop=True,
-                    **token_operand(PACK * g + 2 * u + e)
+                    h[:, j, :], rhs=wv_w[:, cols].bitcast(FP8X4), rhs_scale=wv_s[:, cols], start=True, stop=True,
+                    **token_operand(PACK * g + j)
                 )
-            for e in range(2):
-                j = 2 * u + e
-                nc.scalar.activation(
-                    h_rows[g][:, j, :], h[:, e, :], ACT.Copy, scale=token_cols[:, GROUPS + g, j : j + 1]
-                )
-
-        def weave_h(g):
-            nc.vector.tensor_copy(
-                h_woven[g][:].rearrange("p (c i) j -> p c j i", i=4), h_rows[g][:].rearrange("p j (c i) -> p c j i", i=4)
-            )
-
-        def weights_on(engine, s):
-            g, j = divmod(s, PACK)
-            engine.tensor_scalar(
-                a_rows[g][:, :, j, :],
-                ex[s][:].rearrange("p (c v) -> p c v", c=2),
-                column(recip, s),
-                token_cols[:, g, j : j + 1],
-                ALU.mult,
+            if u == 0:
+                h_woven[g] = sb("h_woven%d" % g, [P, N, PACK], BF16)
+            nc.vector.tensor_tensor(
+                h_woven[g][:, cols, :],
+                h[:].rearrange("p j m -> p m j"),
+                token_cols[:, GROUPS + g, :].unsqueeze(1).to_broadcast([P, P, PACK]),
                 ALU.mult,
             )
 
         def reciprocals(u):
-            nc.vector.reciprocal(recip[batches[u]][:], total[batches[u]][:])
+            nc.vector.reciprocal(recip[u][:], total[u][:])
 
-        def factors(u):
-            batch = batches[u]
-            g, j = divmod(batch[0], PACK)
-            nc.vector.tensor_tensor(factor[batch][:], recip[batch][:], token_cols[:, g, j : j + len(batch)], ALU.mult)
-
-        def weights(s, halves):
+        def weights_on_gpsimd(s):
             g, j = divmod(s, PACK)
-            nc.scalar.activation(
-                a_rows[g][:, halves, j, :],
-                ex[s][:].rearrange("p (c v) -> p c v", c=2)[:, halves, :],
-                ACT.Copy,
-                scale=column(factor, s),
-            )
+            rows = a_rows[:, j, :] if g else a_pairs[:, j // 2, :, j % 2]
+            nc.gpsimd.tensor_scalar(rows, ex[s][:], column(recip, s), mask_of(s), ALU.mult, ALU.mult)
 
-        def weave_a(g, lo, hi):
-            c, first = divmod(lo, HALF)
-            nc.vector.tensor_copy(
-                a_woven[g][:, lo:hi, :].rearrange("p (c i) j -> p c j i", i=4),
-                a_rows[g][:, c, :, first : first + hi - lo].rearrange("p j (c i) -> p c j i", i=4),
-            )
+        def factors(s):
+            nc.scalar.activation(factor[s][:], column(recip, s), ACT.Copy, scale=mask_of(s))
 
-        def quantize_a(g, cols):
-            nc.vector.quantize_mx(
-                a_w[g][:, cols].bitcast(FP8X4), a_s[g][:, cols], a_woven[g][:, cols, :].rearrange("p v j -> p (v j)")
-            )
-
-        def quantize_h(g):
-            nc.vector.quantize_mx(h_w[g][:].bitcast(FP8X4), h_s[g][:], h_woven[g][:].rearrange("p m j -> p (m j)"))
+        def weights(s):
+            nc.scalar.activation(a_rows[:, s - PACK, :], ex[s][:], ACT.Copy, scale=factor[s][:])
 
         acc = {}
 
-        def update(g, c):
+        def update(g, c, first):
             lo, hi = CHUNKS[c]
             for mh in range(2):
-                if g == 0:
-                    acc[c, mh] = bank("acc%d_%d" % (c, mh), (6, 7, 0, 1, 2, 3)[2 * c + mh], [P, hi - lo])
+                if first:
+                    acc[c, mh] = bank("acc%d_%d" % (c, mh), (4, 5, 6, 7, 0, 1)[2 * c + mh], [P, hi - lo])
                 cols = slice(mh * P, (mh + 1) * P)
                 nc.tensor.matmul_mx(
                     acc[c, mh][:],
@@ -234,8 +203,8 @@ def tile_picked_yslot_soft_p_kernel(
                     lhsT_scale=h_s[g][:, cols],
                     rhs=a_w[g][:, lo:hi].bitcast(FP8X4),
                     rhs_scale=a_s[g][:, lo:hi],
-                    start=(g == 0),
-                    stop=(g == GROUPS - 1),
+                    start=first,
+                    stop=not first,
                 )
 
         def store(c, copies, queue):
@@ -245,47 +214,75 @@ def tile_picked_yslot_soft_p_kernel(
                 copies[mh](result[:, mh, :], acc[c, mh][:])
             queue.dma_start(out[:, lo:hi].rearrange("(h p) v -> p h v", p=P), result[:])
 
+        def weave_half(u):
+            a_half[u] = sb("a_half%d" % u, [P, HALF, PACK], BF16)
+            weave(
+                nc.vector.tensor_copy,
+                a_half[u][:].bitcast(I32),
+                a_pairs[:].rearrange("p u v e -> p u (v e)").bitcast(I32)[:, :, u * HALF : (u + 1) * HALF],
+            )
+
+        def quantize_half(u):
+            cols = slice(u * HALF, (u + 1) * HALF)
+            quantize(a_w[0][:, cols], a_s[0][:, cols], a_half[u][:])
+
+        def weave_chunk(copy, c):
+            lo, hi = CHUNKS[c]
+            a_chunk[c] = sb("a_chunk%d" % c, [P, hi - lo, PACK], BF16)
+            weave(copy, a_chunk[c][:], a_rows[:, :, lo:hi])
+
+        def quantize_chunk(c):
+            lo, hi = CHUNKS[c]
+            quantize(a_w[1][:, lo:hi], a_s[1][:, lo:hi], a_chunk[c][:])
+
         gather_slots()
-        gather_tokens(0, None)
-        logits(0)
-        gather_tokens(1, None)
-        logits(1)
-        prepare_wv()
-        logits(2)
+        gather_tokens(0)
+        gather_tokens(1)
+        weave(nc.scalar.copy, wv_bf[:], wv_raw[:])
+        quantize(wv_w[:], wv_s[:], wv_bf[:])
+        for s in range(3):
+            logits(s, s)
         reciprocals(0)
-        weights_on(nc.gpsimd, 0)
-        weights_on(nc.gpsimd, 1)
-        for s in range(3, tiles):
-            logits(s)
+        weights_on_gpsimd(0)
+        logits(3, 3)
+        logits(4, 4)
         reciprocals(1)
-        for g in range(GROUPS):
-            values(g, 0)
-            values(g, 1)
-        weights_on(nc.vector, 2)
+        weights_on_gpsimd(1)
+        weights_on_gpsimd(2)
+        logits(5, 5)
+        logits(6, 6)
         reciprocals(2)
-        weights_on(nc.vector, 3)
-        factors(2)
-        for c in range(2):
-            for s in range(PACK, tiles):
-                weights(s, slice(c, c + 1))
-        weave_h(0)
-        weave_a(0, 0, HALF)
-        quantize_h(0)
-        weave_a(0, HALF, V)
-        quantize_a(0, slice(0, V))
-        weave_h(1)
+        factors(5)
+        logits(7, 7)
+        weights_on_gpsimd(3)
+        weights_on_gpsimd(4)
+        values(0, 0, 0)
+        reciprocals(3)
+        values(0, 1, 1)
+        values(1, 0, 2)
+        values(1, 1, 3)
+        weights(5)
+        factors(6)
+        factors(7)
+        weights(6)
+        weights(7)
         for c in range(len(CHUNKS)):
-            update(0, c)
-        weave_a(1, *CHUNKS[0])
-        quantize_h(1)
-        weave_a(1, *CHUNKS[1])
-        quantize_a(1, slice(*CHUNKS[0]))
-        update(1, 0)
-        weave_a(1, *CHUNKS[2])
-        quantize_a(1, slice(*CHUNKS[1]))
-        update(1, 1)
-        quantize_a(1, slice(*CHUNKS[2]))
-        update(1, 2)
+            weave_chunk(nc.scalar.copy, c)
+        quantize(h_w[0][:], h_s[0][:], h_woven[0][:])
+        weave_half(0)
+        quantize(h_w[1][:], h_s[1][:], h_woven[1][:])
+        quantize_half(0)
+        update(0, 0, True)
+        weave_half(1)
+        quantize_chunk(0)
+        update(1, 0, False)
+        quantize_half(1)
+        update(0, 1, True)
+        update(0, 2, True)
+        quantize_chunk(1)
+        update(1, 1, False)
+        quantize_chunk(2)
+        update(1, 2, False)
         store(0, (nc.scalar.copy, nc.scalar.copy), nc.sync)
         store(1, (nc.scalar.copy, nc.scalar.copy), nc.sync)
         store(2, (nc.scalar.copy, nc.vector.tensor_copy), nc.sync)

@@ -51,7 +51,7 @@ def tile_picked_yslot_soft_p_kernel(
         wv_raw = sb("wv_raw", [P, PACK, N], F32)
         token_list = sb("token_list", [TOKEN_ROWS, PASS], F32)
         token_rows = sb("token_rows", [P, PACK, P], F32)
-        token_cols = sb("token_cols", [P, TOKEN_ROWS, PACK], F32)
+        token_cols = sb("token_cols", [P, TOKEN_ROWS - 1, PACK], F32)
         identity = sb("identity", [P, P], F32)
 
         scales = sb("scales", [P, S + V], U8)
@@ -78,7 +78,9 @@ def tile_picked_yslot_soft_p_kernel(
         turned = bank("turned", 7, [P, PACK, P])
         for j in range(PACK):
             nc.tensor.transpose(turned[:, j, :], token_rows[:, j, :], identity[:])
-        nc.scalar.activation(token_cols[:], turned[:, :, 0:TOKEN_ROWS].rearrange("p j r -> p r j"), ACT.Copy)
+        nc.scalar.activation(token_cols[:], turned[:, :, 0 : TOKEN_ROWS - 1].rearrange("p j r -> p r j"), ACT.Copy)
+        inv_last = sb("inv_last", [P, PACK], F32, "a_first")
+        nc.scalar.activation(inv_last[:], turned[:, :, TOKEN_ROWS - 1], ACT.Copy)
 
         xs_list = sb("xs_list", [P, S], U8)
         es_list = sb("es_list", [P, V], U8)
@@ -93,7 +95,7 @@ def tile_picked_yslot_soft_p_kernel(
             xs_list[:].bitcast(I32).rearrange("p (g b j w) -> p g j b w", g=GROUPS, j=PACK, w=RUN // 4),
         )
         nc.vector.tensor_copy(dealt[:, S : S + V].bitcast(I32), es_list[:].bitcast(I32))
-        for q in range(4):
+        for q in (0, 2, 1, 3):
             nc.sync.dma_start(
                 scales[32 * q : 32 * q + 4, :].bitcast(I32),
                 dealt[FREE_ROWS + 4 * q : FREE_ROWS + 4 * q + 4, :].bitcast(I32),
@@ -142,7 +144,7 @@ def tile_picked_yslot_soft_p_kernel(
         h_s = [sb("h_s%d" % g, [P, N], U8) for g in range(GROUPS)]
         a_w = [sb("a_w%d" % g, [P, V], U32) for g in range(GROUPS)]
         a_s = [sb("a_s%d" % g, [P, V], U8) for g in range(GROUPS)]
-        a_half = {}
+        a_first = []
         a_chunk = {}
 
         def column(tiles, s, n=1):
@@ -171,7 +173,7 @@ def tile_picked_yslot_soft_p_kernel(
             nc.vector.tensor_tensor(
                 h_woven[g][:, cols, :],
                 h[:].rearrange("p j m -> p m j"),
-                token_cols[:, GROUPS + g, :].unsqueeze(1).to_broadcast([P, P, PACK]),
+                (inv_last[:] if g else token_cols[:, GROUPS, :]).unsqueeze(1).to_broadcast([P, P, PACK]),
                 ALU.mult,
             )
 
@@ -207,24 +209,26 @@ def tile_picked_yslot_soft_p_kernel(
                     stop=not first,
                 )
 
-        def store(c, copies, queue):
+        def store(c, halves, copies, tag):
             lo, hi = CHUNKS[c]
-            result = sb("result%d" % c, [P, 2, hi - lo], F32)
-            for mh in range(2):
-                copies[mh](result[:, mh, :], acc[c, mh][:])
-            queue.dma_start(out[:, lo:hi].rearrange("(h p) v -> p h v", p=P), result[:])
+            result = sb("result%d_%d" % (c, halves[0]), [P, len(halves), hi - lo], F32, tag)
+            for e, mh in enumerate(halves):
+                copies[e](result[:, e, :], acc[c, mh][:])
+            rows = out[halves[0] * P : (halves[-1] + 1) * P, lo:hi]
+            nc.sync.dma_start(rows.rearrange("(h p) v -> p h v", p=P), result[:])
 
         def weave_half(u):
-            a_half[u] = sb("a_half%d" % u, [P, HALF, PACK], BF16)
+            if u == 0:
+                a_first.append(sb("a_first", [P, V, PACK], BF16))
             weave(
                 nc.vector.tensor_copy,
-                a_half[u][:].bitcast(I32),
+                a_first[0][:, u * HALF : (u + 1) * HALF, :].bitcast(I32),
                 a_pairs[:].rearrange("p u v e -> p u (v e)").bitcast(I32)[:, :, u * HALF : (u + 1) * HALF],
             )
 
         def quantize_half(u):
             cols = slice(u * HALF, (u + 1) * HALF)
-            quantize(a_w[0][:, cols], a_s[0][:, cols], a_half[u][:])
+            quantize(a_w[0][:, cols], a_s[0][:, cols], a_first[0][:, cols, :])
 
         def weave_chunk(copy, c):
             lo, hi = CHUNKS[c]
@@ -268,21 +272,22 @@ def tile_picked_yslot_soft_p_kernel(
         weights(7)
         for c in range(len(CHUNKS)):
             weave_chunk(nc.scalar.copy, c)
-        quantize(h_w[0][:], h_s[0][:], h_woven[0][:])
         weave_half(0)
-        quantize(h_w[1][:], h_s[1][:], h_woven[1][:])
+        quantize(h_w[0][:], h_s[0][:], h_woven[0][:])
         quantize_half(0)
         update(0, 0, True)
         weave_half(1)
-        quantize_chunk(0)
-        update(1, 0, False)
+        quantize(h_w[1][:], h_s[1][:], h_woven[1][:])
         quantize_half(1)
         update(0, 1, True)
         update(0, 2, True)
+        quantize_chunk(0)
+        update(1, 0, False)
         quantize_chunk(1)
         update(1, 1, False)
         quantize_chunk(2)
         update(1, 2, False)
-        store(0, (nc.scalar.copy, nc.scalar.copy), nc.sync)
-        store(1, (nc.scalar.copy, nc.scalar.copy), nc.sync)
-        store(2, (nc.scalar.copy, nc.vector.tensor_copy), nc.sync)
+        store(0, (0,), (nc.scalar.copy,), None)
+        store(0, (1,), (nc.scalar.copy,), None)
+        store(1, (0, 1), (nc.vector.tensor_copy, nc.vector.tensor_copy), "a_chunk2")
+        store(2, (0, 1), (nc.scalar.copy, nc.vector.tensor_copy), None)

@@ -132,10 +132,9 @@ def tile_picked_yslot_soft_p_kernel(
 
         BATCHES = ((0,), (1, 2), (3, 4, 5), (6, 7))
         neg_max = [sb("neg_max%d" % s, [P, 1], F32) for s in range(TILES)]
-        total = [sb("total%d" % u, [P, len(batch)], F32) for u, batch in enumerate(BATCHES[:-1])]
-        total.append(sb("total3", [P, 2], F32, "h_woven1"))
+        total = [sb("total%d" % u, [P, len(batch)], F32) for u, batch in enumerate(BATCHES)]
         recip = [sb("recip%d" % u, [P, len(batch)], F32) for u, batch in enumerate(BATCHES)]
-        factor = {s: sb("factor%d" % s, [P, 1], F32) for s in (5, 6, 7)}
+        factor = {s: sb("factor%d" % s, [P, 1], F32) for s in (4, 5, 6)}
         ex = [sb("ex%d" % s, [P, V], F32) for s in range(TILES)]
         a_pairs = sb("a_pairs", [P, 2, V, 2], BF16)
         a_rows = sb("a_rows", [P, PACK, V], BF16)
@@ -180,10 +179,10 @@ def tile_picked_yslot_soft_p_kernel(
         def reciprocals(u):
             nc.vector.reciprocal(recip[u][:], total[u][:])
 
-        def weights_on_gpsimd(s):
+        def weights_on(engine, s):
             g, j = divmod(s, PACK)
             rows = a_rows[:, j, :] if g else a_pairs[:, j // 2, :, j % 2]
-            nc.gpsimd.tensor_scalar(rows, ex[s][:], column(recip, s), mask_of(s), ALU.mult, ALU.mult)
+            engine.tensor_scalar(rows, ex[s][:], column(recip, s), mask_of(s), ALU.mult, ALU.mult)
 
         def factors(s):
             nc.scalar.activation(factor[s][:], column(recip, s), ACT.Copy, scale=mask_of(s))
@@ -247,29 +246,29 @@ def tile_picked_yslot_soft_p_kernel(
         for s in range(3):
             logits(s, s)
         reciprocals(0)
-        weights_on_gpsimd(0)
+        weights_on(nc.gpsimd, 0)
         logits(3, 3)
         logits(4, 4)
         reciprocals(1)
-        weights_on_gpsimd(1)
-        weights_on_gpsimd(2)
+        weights_on(nc.gpsimd, 1)
+        weights_on(nc.gpsimd, 2)
         logits(5, 5)
         logits(6, 6)
         reciprocals(2)
+        factors(4)
         factors(5)
         logits(7, 7)
-        weights_on_gpsimd(3)
-        weights_on_gpsimd(4)
+        weights_on(nc.gpsimd, 3)
         values(0, 0, 0)
         reciprocals(3)
         values(0, 1, 1)
         values(1, 0, 2)
         values(1, 1, 3)
+        weights_on(nc.vector, 7)
+        weights(4)
         weights(5)
         factors(6)
-        factors(7)
         weights(6)
-        weights(7)
         for c in range(len(CHUNKS)):
             weave_chunk(nc.scalar.copy, c)
         weave_half(0)

@@ -112,7 +112,6 @@ def tile_picked_yslot_soft_p_kernel(
 
         wv_bf = sb("wv_bf", [P, N, PACK], BF16)
         wv_w = sb("wv_w", [P, N], U32)
-        wv_s = sb("wv_s", [P, N], U8)
 
         def weave(copy, woven, rows):
             copy(woven.rearrange("p (c i) j -> p c j i", i=4), rows.rearrange("p j (c i) -> p c j i", i=4))
@@ -138,9 +137,11 @@ def tile_picked_yslot_soft_p_kernel(
         ex = [sb("ex%d" % s, [P, V], F32) for s in range(TILES)]
         a_pairs = sb("a_pairs", [P, 2, V, 2], BF16)
         a_rows = sb("a_rows", [P, PACK, V], BF16)
-        h_woven = {}
-        h_w = [sb("h_w%d" % g, [P, N], U32) for g in range(GROUPS)]
-        h_s = [sb("h_s%d" % g, [P, N], U8) for g in range(GROUPS)]
+        h_woven = sb("h_woven", [P, GROUPS, N, PACK], BF16)
+        h_words = sb("h_words", [P, GROUPS * N], U32)
+        h_scales = sb("h_scales", [P, GROUPS * N], U8)
+        h_w = [h_words[:, g * N : (g + 1) * N] for g in range(GROUPS)]
+        h_s = [h_scales[:, g * N : (g + 1) * N] for g in range(GROUPS)]
         a_w = [sb("a_w%d" % g, [P, V], U32) for g in range(GROUPS)]
         a_s = [sb("a_s%d" % g, [P, V], U8) for g in range(GROUPS)]
         a_first = []
@@ -167,10 +168,8 @@ def tile_picked_yslot_soft_p_kernel(
                     h[:, j, :], rhs=wv_w[:, cols].bitcast(FP8X4), rhs_scale=wv_s[:, cols], start=True, stop=True,
                     **token_operand(PACK * g + j)
                 )
-            if u == 0:
-                h_woven[g] = sb("h_woven%d" % g, [P, N, PACK], BF16)
             nc.vector.tensor_tensor(
-                h_woven[g][:, cols, :],
+                h_woven[:, g, cols, :],
                 h[:].rearrange("p j m -> p m j"),
                 (inv_last[:] if g else token_cols[:, GROUPS, :]).unsqueeze(1).to_broadcast([P, P, PACK]),
                 ALU.mult,
@@ -242,11 +241,13 @@ def tile_picked_yslot_soft_p_kernel(
         gather_tokens(0)
         gather_tokens(1)
         weave(nc.scalar.copy, wv_bf[:], wv_raw[:])
+        logits(0, 0)
+        logits(1, 1)
+        wv_s = sb("wv_s", [P, N], U8, "neg_max0")
         quantize(wv_w[:], wv_s[:], wv_bf[:])
-        for s in range(3):
-            logits(s, s)
         reciprocals(0)
         weights_on(nc.gpsimd, 0)
+        logits(2, 2)
         logits(3, 3)
         logits(4, 4)
         reciprocals(1)
@@ -272,11 +273,10 @@ def tile_picked_yslot_soft_p_kernel(
         for c in range(len(CHUNKS)):
             weave_chunk(nc.scalar.copy, c)
         weave_half(0)
-        quantize(h_w[0][:], h_s[0][:], h_woven[0][:])
+        quantize(h_words[:], h_scales[:], h_woven[:].rearrange("p g m j -> p (g m) j"))
+        weave_half(1)
         quantize_half(0)
         update(0, 0, True)
-        weave_half(1)
-        quantize(h_w[1][:], h_s[1][:], h_woven[1][:])
         quantize_half(1)
         update(0, 1, True)
         update(0, 2, True)

@@ -51,7 +51,7 @@ def tile_picked_yslot_soft_p_kernel(
         wv_raw = sb("wv_raw", [P, PACK, N], F32)
         token_list = sb("token_list", [TOKEN_ROWS, PASS], F32)
         token_rows = sb("token_rows", [P, PACK, P], F32)
-        token_cols = sb("token_cols", [P, TOKEN_ROWS - 1, PACK], F32)
+        token_cols = sb("token_cols", [P, TOKEN_ROWS, PACK], F32)
         identity = sb("identity", [P, P], F32)
 
         scales = sb("scales", [P, S + V], U8)
@@ -78,9 +78,7 @@ def tile_picked_yslot_soft_p_kernel(
         turned = bank("turned", 7, [P, PACK, P])
         for j in range(PACK):
             nc.tensor.transpose(turned[:, j, :], token_rows[:, j, :], identity[:])
-        nc.scalar.activation(token_cols[:], turned[:, :, 0 : TOKEN_ROWS - 1].rearrange("p j r -> p r j"), ACT.Copy)
-        inv_last = sb("inv_last", [P, PACK], F32, "a_first")
-        nc.scalar.activation(inv_last[:], turned[:, :, TOKEN_ROWS - 1], ACT.Copy)
+        nc.scalar.activation(token_cols[:], turned[:, :, 0:TOKEN_ROWS].rearrange("p j r -> p r j"), ACT.Copy)
 
         xs_list = sb("xs_list", [P, S], U8)
         es_list = sb("es_list", [P, V], U8)
@@ -133,10 +131,9 @@ def tile_picked_yslot_soft_p_kernel(
         neg_max = [sb("neg_max%d" % s, [P, 1], F32) for s in range(TILES)]
         total = [sb("total%d" % u, [P, len(batch)], F32) for u, batch in enumerate(BATCHES)]
         recip = [sb("recip%d" % u, [P, len(batch)], F32) for u, batch in enumerate(BATCHES)]
-        factor = {s: sb("factor%d" % s, [P, 1], F32) for s in (4, 5, 6)}
+        factor = {s: sb("factor%d" % s, [P, 1], F32) for s in (4, 5)}
         ex = [sb("ex%d" % s, [P, V], F32) for s in range(TILES)]
-        a_pairs = sb("a_pairs", [P, 2, V, 2], BF16)
-        a_rows = sb("a_rows", [P, PACK, V], BF16)
+        a_pairs = [sb("a_pairs%d" % g, [P, 2, V, 2], BF16) for g in range(GROUPS)]
         h_woven = sb("h_woven", [P, GROUPS, N, PACK], BF16)
         h_words = sb("h_words", [P, GROUPS * N], U32)
         h_scales = sb("h_scales", [P, GROUPS * N], U8)
@@ -144,7 +141,7 @@ def tile_picked_yslot_soft_p_kernel(
         h_s = [h_scales[:, g * N : (g + 1) * N] for g in range(GROUPS)]
         a_w = [sb("a_w%d" % g, [P, V], U32) for g in range(GROUPS)]
         a_s = [sb("a_s%d" % g, [P, V], U8) for g in range(GROUPS)]
-        a_first = []
+        a_half = {}
         a_chunk = {}
 
         def column(tiles, s, n=1):
@@ -171,23 +168,28 @@ def tile_picked_yslot_soft_p_kernel(
             nc.vector.tensor_tensor(
                 h_woven[:, g, cols, :],
                 h[:].rearrange("p j m -> p m j"),
-                (inv_last[:] if g else token_cols[:, GROUPS, :]).unsqueeze(1).to_broadcast([P, P, PACK]),
+                token_cols[:, GROUPS + g, :].unsqueeze(1).to_broadcast([P, P, PACK]),
                 ALU.mult,
             )
 
         def reciprocals(u):
             nc.vector.reciprocal(recip[u][:], total[u][:])
 
-        def weights_on(engine, s):
+        def rows_of(s):
             g, j = divmod(s, PACK)
-            rows = a_rows[:, j, :] if g else a_pairs[:, j // 2, :, j % 2]
-            engine.tensor_scalar(rows, ex[s][:], column(recip, s), mask_of(s), ALU.mult, ALU.mult)
+            return a_pairs[g][:, j // 2, :, j % 2]
+
+        def words_of(g, lo, hi):
+            return a_pairs[g][:].rearrange("p u v e -> p u (v e)").bitcast(U32)[:, :, lo:hi]
+
+        def weights_on(engine, s):
+            engine.tensor_scalar(rows_of(s), ex[s][:], column(recip, s), mask_of(s), ALU.mult, ALU.mult)
 
         def factors(s):
             nc.scalar.activation(factor[s][:], column(recip, s), ACT.Copy, scale=mask_of(s))
 
         def weights(s):
-            nc.scalar.activation(a_rows[:, s - PACK, :], ex[s][:], ACT.Copy, scale=factor[s][:])
+            nc.scalar.activation(rows_of(s), ex[s][:], ACT.Copy, scale=factor[s][:])
 
         acc = {}
 
@@ -216,22 +218,17 @@ def tile_picked_yslot_soft_p_kernel(
             nc.sync.dma_start(rows.rearrange("(h p) v -> p h v", p=P), result[:])
 
         def weave_half(u):
-            if u == 0:
-                a_first.append(sb("a_first", [P, V, PACK], BF16))
-            weave(
-                nc.vector.tensor_copy,
-                a_first[0][:, u * HALF : (u + 1) * HALF, :].bitcast(I32),
-                a_pairs[:].rearrange("p u v e -> p u (v e)").bitcast(I32)[:, :, u * HALF : (u + 1) * HALF],
-            )
+            a_half[u] = sb("a_half%d" % u, [P, HALF, PACK], BF16, "ex7" if u else None)
+            weave(nc.scalar.copy, a_half[u][:].bitcast(U32), words_of(0, u * HALF, (u + 1) * HALF))
 
         def quantize_half(u):
             cols = slice(u * HALF, (u + 1) * HALF)
-            quantize(a_w[0][:, cols], a_s[0][:, cols], a_first[0][:, cols, :])
+            quantize(a_w[0][:, cols], a_s[0][:, cols], a_half[u][:])
 
         def weave_chunk(copy, c):
             lo, hi = CHUNKS[c]
             a_chunk[c] = sb("a_chunk%d" % c, [P, hi - lo, PACK], BF16)
-            weave(copy, a_chunk[c][:], a_rows[:, :, lo:hi])
+            weave(copy, a_chunk[c][:].bitcast(U32), words_of(1, lo, hi))
 
         def quantize_chunk(c):
             lo, hi = CHUNKS[c]
@@ -265,23 +262,23 @@ def tile_picked_yslot_soft_p_kernel(
         values(0, 1, 1)
         values(1, 0, 2)
         values(1, 1, 3)
+        weights_on(nc.vector, 6)
         weights_on(nc.vector, 7)
         weights(4)
         weights(5)
-        factors(6)
-        weights(6)
-        for c in range(len(CHUNKS)):
-            weave_chunk(nc.scalar.copy, c)
         weave_half(0)
-        quantize(h_words[:], h_scales[:], h_woven[:].rearrange("p g m j -> p (g m) j"))
+        weave_chunk(nc.scalar.copy, 0)
         weave_half(1)
+        weave_chunk(nc.scalar.copy, 1)
+        weave_chunk(nc.scalar.copy, 2)
+        quantize(h_words[:], h_scales[:], h_woven[:].rearrange("p g m j -> p (g m) j"))
         quantize_half(0)
         update(0, 0, True)
+        quantize_chunk(0)
+        update(1, 0, False)
         quantize_half(1)
         update(0, 1, True)
         update(0, 2, True)
-        quantize_chunk(0)
-        update(1, 0, False)
         quantize_chunk(1)
         update(1, 1, False)
         quantize_chunk(2)

@@ -166,9 +166,9 @@ def tile_picked_yslot_soft_p_kernel(
                     **token_operand(PACK * g + j)
                 )
             nc.vector.tensor_tensor(
-                h_woven[:, g, cols, :],
-                h[:].rearrange("p j m -> p m j"),
-                token_cols[:, GROUPS + g, :].unsqueeze(1).to_broadcast([P, P, PACK]),
+                h_woven[:, g, cols, :].rearrange("p (c i) j -> p c j i", i=2),
+                h[:].rearrange("p j (c i) -> p c j i", i=2),
+                token_cols[:, GROUPS + g, :].unsqueeze(1).unsqueeze(3).to_broadcast([P, P // 2, PACK, 2]),
                 ALU.mult,
             )
 
@@ -241,8 +241,8 @@ def tile_picked_yslot_soft_p_kernel(
         logits(0, 0)
         logits(1, 1)
         wv_s = sb("wv_s", [P, N], U8, "neg_max0")
-        quantize(wv_w[:], wv_s[:], wv_bf[:])
         reciprocals(0)
+        quantize(wv_w[:], wv_s[:], wv_bf[:])
         weights_on(nc.gpsimd, 0)
         logits(2, 2)
         logits(3, 3)
@@ -264,6 +264,11 @@ def tile_picked_yslot_soft_p_kernel(
         values(1, 1, 3)
         weights_on(nc.vector, 6)
         weights_on(nc.vector, 7)
+        warm = bank("warm", 2, [P, V])
+        for s in range(3):
+            nc.tensor.matmul_mx(
+                warm[:], rhs=ew[:].bitcast(FP8X4), rhs_scale=scales[:, S : S + V], start=True, stop=True, **token_operand(s)
+            )
         weights(4)
         weights(5)
         weave_half(0)

@@ -209,11 +209,12 @@ def tile_picked_yslot_soft_p_kernel(
                     stop=not first,
                 )
 
-        def store(c, halves, copies, tag):
-            lo, hi = CHUNKS[c]
-            result = sb("result%d_%d" % (c, halves[0]), [P, len(halves), hi - lo], F32, tag)
-            for e, mh in enumerate(halves):
-                copies[e](result[:, e, :], acc[c, mh][:])
+        def store(chunks, halves, copies, tag):
+            lo, hi = CHUNKS[chunks[0]][0], CHUNKS[chunks[-1]][1]
+            result = sb("result%d_%d" % (chunks[0], halves[0]), [P, len(halves), hi - lo], F32, tag)
+            for c in chunks:
+                for e, mh in enumerate(halves):
+                    copies[e](result[:, e, CHUNKS[c][0] - lo : CHUNKS[c][1] - lo], acc[c, mh][:])
             rows = out[halves[0] * P : (halves[-1] + 1) * P, lo:hi]
             nc.sync.dma_start(rows.rearrange("(h p) v -> p h v", p=P), result[:])
 
@@ -288,7 +289,6 @@ def tile_picked_yslot_soft_p_kernel(
         update(1, 1, False)
         quantize_chunk(2)
         update(1, 2, False)
-        store(0, (0,), (nc.scalar.copy,), None)
-        store(0, (1,), (nc.scalar.copy,), None)
-        store(1, (0, 1), (nc.vector.tensor_copy, nc.vector.tensor_copy), "a_chunk2")
-        store(2, (0, 1), (nc.scalar.copy, nc.vector.tensor_copy), None)
+        store((0,), (0,), (nc.scalar.copy,), None)
+        store((0,), (1,), (nc.scalar.copy,), None)
+        store((1, 2), (0, 1), (nc.scalar.copy, nc.vector.tensor_copy), "a_chunk2")

@@ -55,14 +55,14 @@ def tile_picked_yslot_soft_p_kernel(
         identity = sb("identity", [P, P], F32)
 
         scales = sb("scales", [P, S + V], U8)
-        nc.vector.memset(xs_all[0:FREE_ROWS, :].bitcast(I32), 0)
+        nc.gpsimd.memset(xs_all[0:FREE_ROWS, :].bitcast(I32), 0)
         nc.vector.memset(es_all[0:FREE_ROWS, :].bitcast(I32), 0)
         nc.vector.memset(scales[:].bitcast(I32), 0)
 
         nc.sync.dma_start(offs_sb[:], offs)
         nc.sync.dma_start(xs_all[FREE_ROWS:P, :].bitcast(I32), x_scales[0].bitcast(I32))
+        nc.scalar.dma_start(es_all[FREE_ROWS:P, :].bitcast(I32), e_scales[0].bitcast(I32))
         nc.sync.dma_start(slot_sb[:], slot)
-        nc.sync.dma_start(es_all[FREE_ROWS:P, :].bitcast(I32), e_scales[0].bitcast(I32))
         nc.sync.dma_start(ew_all[:], e_words[0].rearrange("p n t -> p (n t)").bitcast(I32))
         nc.sync.dma_start(xw_all[:], x_words[0].rearrange("p n t -> p (n t)").bitcast(I32))
         nc.sync.dma_start(wv_raw[:], wv.rearrange("(p j) m -> p j m", j=PACK))
@@ -80,19 +80,17 @@ def tile_picked_yslot_soft_p_kernel(
             nc.tensor.transpose(turned[:, j, :], token_rows[:, j, :], identity[:])
         nc.scalar.activation(token_cols[:], turned[:, :, 0:TOKEN_ROWS].rearrange("p j r -> p r j"), ACT.Copy)
 
-        xs_list = sb("xs_list", [P, S], U8)
-        es_list = sb("es_list", [P, V], U8)
+        listed = sb("listed", [P, S + V], U8)
         dealt = sb("dealt", [P, S + V], U8)
-        xw = [sb("xw%d" % g, [P, PASS], U32) for g in range(GROUPS)]
+        xw = {}
         ew = sb("ew", [P, V], U32)
 
-        nc.vector.tensor_copy(xs_list[:], xs_all[:].indirect(offs_sb[:]))
-        nc.vector.tensor_copy(es_list[:], es_all[:].indirect(slot_sb[:]))
+        nc.vector.tensor_copy(listed[:, 0:S], xs_all[:].indirect(offs_sb[:]))
+        nc.vector.tensor_copy(listed[:, S : S + V], es_all[:].indirect(slot_sb[:]))
         nc.vector.tensor_copy(
-            dealt[:, 0:S].bitcast(I32).rearrange("p (g j b w) -> p g j b w", g=GROUPS, j=PACK, w=RUN // 4),
-            xs_list[:].bitcast(I32).rearrange("p (g b j w) -> p g j b w", g=GROUPS, j=PACK, w=RUN // 4),
+            dealt[:].bitcast(I32).rearrange("p (g j b w) -> p g j b w", g=GROUPS + 1, j=PACK, w=RUN // 4),
+            listed[:].bitcast(I32).rearrange("p (g b j w) -> p g j b w", g=GROUPS + 1, j=PACK, w=RUN // 4),
         )
-        nc.vector.tensor_copy(dealt[:, S : S + V].bitcast(I32), es_list[:].bitcast(I32))
         for q in (0, 2, 1, 3):
             nc.sync.dma_start(
                 scales[32 * q : 32 * q + 4, :].bitcast(I32),
@@ -100,9 +98,12 @@ def tile_picked_yslot_soft_p_kernel(
             )
 
         def gather_slots():
-            nc.vector.tensor_copy(ew[:], ew_all[:].bitcast(U32).indirect(slot_sb[:]))
+            nc.vector.tensor_copy(
+                ew[:].rearrange("p (j b i) -> p b j i", j=PACK, i=RUN), ew_all[:].bitcast(U32).indirect(slot_sb[:])
+            )
 
         def gather_tokens(g):
+            xw[g] = sb("xw%d" % g, [P, PASS], U32)
             nc.vector.tensor_copy(
                 xw[g][:].rearrange("p (j b i) -> p b j i", j=PACK, i=RUN),
                 xw_all[:].bitcast(U32).indirect(offs_sb[:, g * PASS // 16 : (g + 1) * PASS // 16]),
@@ -155,7 +156,13 @@ def tile_picked_yslot_soft_p_kernel(
                 y[:], rhs=ew[:].bitcast(FP8X4), rhs_scale=scales[:, S : S + V], start=True, stop=True, **token_operand(s)
             )
             nc.vector.tensor_reduce(neg_max[s][:], y[:], mybir.AxisListType.X, ALU.max, negate=True)
-            nc.scalar.activation(ex[s][:], y[:], ACT.Exp, bias=neg_max[s][:], accum_out=column(total, s))
+            nc.scalar.activation(
+                ex[s][:].rearrange("p (b j i) -> p j b i", j=PACK, i=RUN),
+                y[:].rearrange("p (j b i) -> p j b i", j=PACK, i=RUN),
+                ACT.Exp,
+                bias=neg_max[s][:],
+                accum_out=column(total, s),
+            )
 
         def values(g, u, number):
             h = bank("h%d_%d" % (g, u), number, [P, PACK, P])
@@ -265,11 +272,6 @@ def tile_picked_yslot_soft_p_kernel(
         values(1, 1, 3)
         weights_on(nc.vector, 6)
         weights_on(nc.vector, 7)
-        warm = bank("warm", 2, [P, V])
-        for s in range(3):
-            nc.tensor.matmul_mx(
-                warm[:], rhs=ew[:].bitcast(FP8X4), rhs_scale=scales[:, S : S + V], start=True, stop=True, **token_operand(s)
-            )
         weights(4)
         weights(5)
         weave_half(0)
@@ -289,6 +291,6 @@ def tile_picked_yslot_soft_p_kernel(
         update(1, 1, False)
         quantize_chunk(2)
         update(1, 2, False)
-        store((0,), (0,), (nc.scalar.copy,), None)
-        store((0,), (1,), (nc.scalar.copy,), None)
-        store((1, 2), (0, 1), (nc.scalar.copy, nc.vector.tensor_copy), "a_chunk2")
+        store((0,), (0, 1), (nc.scalar.copy, nc.vector.tensor_copy), None)
+        store((1,), (0, 1), (nc.scalar.copy, nc.scalar.copy), None)
+        store((2,), (0, 1), (nc.scalar.copy, nc.vector.tensor_copy), None)

@@ -134,8 +134,9 @@ def tile_picked_yslot_soft_p_kernel(
         recip = [sb("recip%d" % u, [P, len(batch)], F32) for u, batch in enumerate(BATCHES)]
         factor = {s: sb("factor%d" % s, [P, 1], F32) for s in (4, 5)}
         ex = [sb("ex%d" % s, [P, V], F32) for s in range(TILES)]
-        a_pairs = [sb("a_pairs%d" % g, [P, 2, V, 2], BF16) for g in range(GROUPS)]
-        h_woven = sb("h_woven", [P, GROUPS, N, PACK], BF16)
+        PARTS = (1, 2)
+        a_pairs = [sb("a_pairs%d" % g, [P, n, 2, V // n, 2], BF16) for g, n in enumerate(PARTS)]
+        h_woven = [sb("h_woven%d" % g, [P, N, PACK], BF16) for g in range(GROUPS)]
         h_words = sb("h_words", [P, GROUPS * N], U32)
         h_scales = sb("h_scales", [P, GROUPS * N], U8)
         h_w = [h_words[:, g * N : (g + 1) * N] for g in range(GROUPS)]
@@ -173,7 +174,7 @@ def tile_picked_yslot_soft_p_kernel(
                     **token_operand(PACK * g + j)
                 )
             nc.vector.tensor_tensor(
-                h_woven[:, g, cols, :].rearrange("p (c i) j -> p c j i", i=2),
+                h_woven[g][:, cols, :].rearrange("p (c i) j -> p c j i", i=2),
                 h[:].rearrange("p j (c i) -> p c j i", i=2),
                 token_cols[:, GROUPS + g, :].unsqueeze(1).unsqueeze(3).to_broadcast([P, P // 2, PACK, 2]),
                 ALU.mult,
@@ -184,19 +185,29 @@ def tile_picked_yslot_soft_p_kernel(
 
         def rows_of(s):
             g, j = divmod(s, PACK)
-            return a_pairs[g][:, j // 2, :, j % 2]
+            return a_pairs[g][:, :, j // 2, :, j % 2]
 
         def words_of(g, lo, hi):
-            return a_pairs[g][:].rearrange("p u v e -> p u (v e)").bitcast(U32)[:, :, lo:hi]
+            part, first = divmod(lo, V // PARTS[g])
+            words = a_pairs[g][:, part].rearrange("p u v e -> p u (v e)").bitcast(U32)
+            return words[:, :, first : first + hi - lo]
+
+        def halves_of(s):
+            return ex[s][:].rearrange("p (h v) -> p h v", h=PARTS[s // PACK])
 
         def weights_on(engine, s):
-            engine.tensor_scalar(rows_of(s), ex[s][:], column(recip, s), mask_of(s), ALU.mult, ALU.mult)
+            engine.tensor_scalar(rows_of(s), halves_of(s), column(recip, s), mask_of(s), ALU.mult, ALU.mult)
+
+        def half_weights(s, u):
+            nc.vector.tensor_scalar(
+                rows_of(s)[:, u], halves_of(s)[:, u], column(recip, s), mask_of(s), ALU.mult, ALU.mult
+            )
 
         def factors(s):
             nc.scalar.activation(factor[s][:], column(recip, s), ACT.Copy, scale=mask_of(s))
 
         def weights(s):
-            nc.scalar.activation(rows_of(s), ex[s][:], ACT.Copy, scale=factor[s][:])
+            nc.scalar.activation(rows_of(s), halves_of(s), ACT.Copy, scale=factor[s][:])
 
         acc = {}
 
@@ -204,7 +215,7 @@ def tile_picked_yslot_soft_p_kernel(
             lo, hi = CHUNKS[c]
             for mh in range(2):
                 if first:
-                    acc[c, mh] = bank("acc%d_%d" % (c, mh), (4, 5, 6, 7, 0, 1)[2 * c + mh], [P, hi - lo])
+                    acc[c, mh] = bank("acc%d_%d" % (c, mh), (4, 5, 6, 7, 2, 1)[2 * c + mh], [P, hi - lo])
                 cols = slice(mh * P, (mh + 1) * P)
                 nc.tensor.matmul_mx(
                     acc[c, mh][:],
@@ -254,34 +265,43 @@ def tile_picked_yslot_soft_p_kernel(
         weights_on(nc.gpsimd, 0)
         logits(2, 2)
         logits(3, 3)
-        logits(4, 4)
+        logits(4, 0)
         reciprocals(1)
         weights_on(nc.gpsimd, 1)
         weights_on(nc.gpsimd, 2)
-        logits(5, 5)
-        logits(6, 6)
+        logits(5, 1)
+        logits(6, 2)
         reciprocals(2)
         factors(4)
         factors(5)
-        logits(7, 7)
+        logits(7, 3)
         weights_on(nc.gpsimd, 3)
         values(0, 0, 0)
         reciprocals(3)
         values(0, 1, 1)
         values(1, 0, 2)
-        values(1, 1, 3)
-        weights_on(nc.vector, 6)
-        weights_on(nc.vector, 7)
+        values(1, 1, 0)
+        warm = bank("warm", 0, [P, N])
+        for turn in range(3):
+            nc.tensor.matmul_mx(
+                warm[:], lhsT=wv_w[:, 0:P].bitcast(FP8X4), lhsT_scale=wv_s[:, 0:P], rhs=wv_w[:].bitcast(FP8X4),
+                rhs_scale=wv_s[:], start=True, stop=True,
+            )
         weights(4)
         weights(5)
         weave_half(0)
+        quantize(h_w[0], h_s[0], h_woven[0][:])
+        half_weights(6, 0)
+        half_weights(7, 0)
+        quantize_half(0)
+        update(0, 0, True)
+        half_weights(6, 1)
+        half_weights(7, 1)
         weave_chunk(nc.scalar.copy, 0)
         weave_half(1)
         weave_chunk(nc.scalar.copy, 1)
         weave_chunk(nc.scalar.copy, 2)
-        quantize(h_words[:], h_scales[:], h_woven[:].rearrange("p g m j -> p (g m) j"))
-        quantize_half(0)
-        update(0, 0, True)
+        quantize(h_w[1], h_s[1], h_woven[1][:])
         quantize_chunk(0)
         update(1, 0, False)
         quantize_half(1)

@@ -26,6 +26,7 @@ CHUNKS = ((0, 256), (256, 384), (384, 512))
 FREE_ROWS = P - 16
 TOKEN_ROWS = 2 * GROUPS
 TILES = GROUPS * PACK
+LATE = N - 64
 
 
 def tile_picked_yslot_soft_p_kernel(
@@ -165,20 +166,27 @@ def tile_picked_yslot_soft_p_kernel(
                 accum_out=column(total, s),
             )
 
-        def values(g, u, number):
-            h = bank("h%d_%d" % (g, u), number, [P, PACK, P])
-            cols = slice(u * P, (u + 1) * P)
+        h_bank = {}
+
+        def project(g, lo, hi, number):
+            h_bank[g, lo] = bank("h%d_%d" % (g, lo), number, [P, PASS])
             for j in range(PACK):
                 nc.tensor.matmul_mx(
-                    h[:, j, :], rhs=wv_w[:, cols].bitcast(FP8X4), rhs_scale=wv_s[:, cols], start=True, stop=True,
-                    **token_operand(PACK * g + j)
+                    h_bank[g, lo][:, j * (hi - lo) : (j + 1) * (hi - lo)], rhs=wv_w[:, lo:hi].bitcast(FP8X4),
+                    rhs_scale=wv_s[:, lo:hi], start=True, stop=True, **token_operand(PACK * g + j)
                 )
+
+        def scale_values(g, lo, hi):
             nc.vector.tensor_tensor(
-                h_woven[g][:, cols, :].rearrange("p (c i) j -> p c j i", i=2),
-                h[:].rearrange("p j (c i) -> p c j i", i=2),
-                token_cols[:, GROUPS + g, :].unsqueeze(1).unsqueeze(3).to_broadcast([P, P // 2, PACK, 2]),
+                h_woven[g][:, lo:hi, :].rearrange("p (c i) j -> p c j i", i=2),
+                h_bank[g, lo][:, 0 : PACK * (hi - lo)].rearrange("p (j c i) -> p c j i", j=PACK, i=2),
+                token_cols[:, GROUPS + g, :].unsqueeze(1).unsqueeze(3).to_broadcast([P, (hi - lo) // 2, PACK, 2]),
                 ALU.mult,
             )
+
+        def values(g, lo, hi, number):
+            project(g, lo, hi, number)
+            scale_values(g, lo, hi)
 
         def reciprocals(u):
             nc.vector.reciprocal(recip[u][:], total[u][:])
@@ -276,15 +284,16 @@ def tile_picked_yslot_soft_p_kernel(
         factors(5)
         logits(7, 3)
         weights_on(nc.gpsimd, 3)
-        values(0, 0, 0)
+        values(0, 0, P, 0)
         reciprocals(3)
-        values(0, 1, 1)
-        values(1, 0, 2)
-        values(1, 1, 0)
-        warm = bank("warm", 0, [P, N])
+        values(0, P, N, 1)
+        values(1, 0, P, 2)
+        values(1, P, LATE, 0)
+        project(1, LATE, N, 0)
+        warm = h_bank[1, LATE][:, N:PASS]
         for turn in range(3):
             nc.tensor.matmul_mx(
-                warm[:], lhsT=wv_w[:, 0:P].bitcast(FP8X4), lhsT_scale=wv_s[:, 0:P], rhs=wv_w[:].bitcast(FP8X4),
+                warm, lhsT=wv_w[:, 0:P].bitcast(FP8X4), lhsT_scale=wv_s[:, 0:P], rhs=wv_w[:].bitcast(FP8X4),
                 rhs_scale=wv_s[:], start=True, stop=True,
             )
         weights(4)
@@ -293,6 +302,7 @@ def tile_picked_yslot_soft_p_kernel(
         quantize(h_w[0], h_s[0], h_woven[0][:])
         half_weights(6, 0)
         half_weights(7, 0)
+        scale_values(1, LATE, N)
         quantize_half(0)
         update(0, 0, True)
         half_weights(6, 1)

@@ -40,22 +40,25 @@ def tile_picked_yslot_soft_p_kernel(
         def sb(name, shape, dtype, tag=None):
             return keep.tile(shape, dtype, name=name, tag=tag or name, align_bytes=64)
 
+        def dma_tile(name, shape, dtype):
+            return keep.tile(shape, dtype, name=name, align_bytes=256)
+
         def bank(name, number, shape):
             return psum.tile(shape, F32, name=name, tag="bank%d" % number)
 
         offs_sb = keep.tile([P, S // 16], U16, name="offs_sb")
         slot_sb = keep.tile([P, V // 16], U16, name="slot_sb")
-        xw_all = sb("xw_all", [P, T], I32)
-        ew_all = sb("ew_all", [P, W], I32)
-        xs_all = sb("xs_all", [P, T], U8)
-        es_all = sb("es_all", [P, W], U8)
-        wv_raw = sb("wv_raw", [P, PACK, N], F32)
-        token_list = sb("token_list", [TOKEN_ROWS, PASS], F32)
+        xw_all = dma_tile("xw_all", [P, T], I32)
+        ew_all = dma_tile("ew_all", [P, W], I32)
+        xs_all = dma_tile("xs_all", [P, T], U8)
+        es_all = dma_tile("es_all", [P, W], U8)
+        wv_raw = dma_tile("wv_raw", [P, PACK, N], F32)
+        token_list = dma_tile("token_list", [TOKEN_ROWS, PASS], F32)
         token_rows = sb("token_rows", [P, PACK, P], F32)
         token_cols = sb("token_cols", [P, TOKEN_ROWS, PACK], F32)
         identity = sb("identity", [P, P], F32)
 
-        scales = sb("scales", [P, S + V], U8)
+        scales = dma_tile("scales", [P, S + V], U8)
         nc.gpsimd.memset(xs_all[0:FREE_ROWS, :].bitcast(I32), 0)
         nc.vector.memset(es_all[0:FREE_ROWS, :].bitcast(I32), 0)
         nc.vector.memset(scales[:].bitcast(I32), 0)
@@ -82,7 +85,7 @@ def tile_picked_yslot_soft_p_kernel(
         nc.scalar.activation(token_cols[:], turned[:, :, 0:TOKEN_ROWS].rearrange("p j r -> p r j"), ACT.Copy)
 
         listed = sb("listed", [P, S + V], U8)
-        dealt = sb("dealt", [P, S + V], U8)
+        dealt = dma_tile("dealt", [P, S + V], U8)
         xw = {}
         ew = sb("ew", [P, V], U32)
 
@@ -235,9 +238,9 @@ def tile_picked_yslot_soft_p_kernel(
                     stop=not first,
                 )
 
-        def store(chunks, halves, copies, tag):
+        def store(chunks, halves, copies):
             lo, hi = CHUNKS[chunks[0]][0], CHUNKS[chunks[-1]][1]
-            result = sb("result%d_%d" % (chunks[0], halves[0]), [P, len(halves), hi - lo], F32, tag)
+            result = dma_tile("result%d_%d" % (chunks[0], halves[0]), [P, len(halves), hi - lo], F32)
             for c in chunks:
                 for e, mh in enumerate(halves):
                     copies[e](result[:, e, CHUNKS[c][0] - lo : CHUNKS[c][1] - lo], acc[c, mh][:])
@@ -321,6 +324,6 @@ def tile_picked_yslot_soft_p_kernel(
         update(1, 1, False)
         quantize_chunk(2)
         update(1, 2, False)
-        store((0,), (0, 1), (nc.scalar.copy, nc.vector.tensor_copy), None)
-        store((1,), (0, 1), (nc.scalar.copy, nc.scalar.copy), None)
-        store((2,), (0, 1), (nc.scalar.copy, nc.vector.tensor_copy), None)
+        store((0,), (0, 1), (nc.scalar.copy, nc.vector.tensor_copy))
+        store((1,), (0, 1), (nc.scalar.copy, nc.scalar.copy))
+        store((2,), (0, 1), (nc.scalar.copy, nc.vector.tensor_copy))

@@ -182,8 +182,8 @@ def tile_picked_yslot_soft_p_kernel(
         def scale_values(g, lo, hi):
             nc.vector.tensor_tensor(
                 h_woven[g][:, lo:hi, :].rearrange("p (c i) j -> p c j i", i=2),
-                h_bank[g, lo][:, 0 : PACK * (hi - lo)].rearrange("p (j c i) -> p c j i", j=PACK, i=2),
                 token_cols[:, GROUPS + g, :].unsqueeze(1).unsqueeze(3).to_broadcast([P, (hi - lo) // 2, PACK, 2]),
+                h_bank[g, lo][:, 0 : PACK * (hi - lo)].rearrange("p (j c i) -> p c j i", j=PACK, i=2),
                 ALU.mult,
             )
 

@@ -243,7 +243,7 @@ def tile_picked_yslot_soft_p_kernel(
             result = dma_tile("result%d_%d" % (chunks[0], halves[0]), [P, len(halves), hi - lo], F32)
             for c in chunks:
                 for e, mh in enumerate(halves):
-                    copies[e](result[:, e, CHUNKS[c][0] - lo : CHUNKS[c][1] - lo], acc[c, mh][:])
+                    copies[c - chunks[0]][e](result[:, e, CHUNKS[c][0] - lo : CHUNKS[c][1] - lo], acc[c, mh][:])
             rows = out[halves[0] * P : (halves[-1] + 1) * P, lo:hi]
             nc.sync.dma_start(rows.rearrange("(h p) v -> p h v", p=P), result[:])
 
@@ -324,6 +324,6 @@ def tile_picked_yslot_soft_p_kernel(
         update(1, 1, False)
         quantize_chunk(2)
         update(1, 2, False)
-        store((0,), (0, 1), (nc.scalar.copy, nc.vector.tensor_copy))
-        store((1,), (0, 1), (nc.scalar.copy, nc.scalar.copy))
-        store((2,), (0, 1), (nc.scalar.copy, nc.vector.tensor_copy))
+        store((0,), (0,), ((nc.scalar.copy,),))
+        store((0,), (1,), ((nc.scalar.copy,),))
+        store((1, 2), (0, 1), ((nc.scalar.copy, nc.vector.tensor_copy), (nc.scalar.copy, nc.vector.tensor_copy)))

@@ -291,8 +291,8 @@ def tile_picked_yslot_soft_p_kernel(
         reciprocals(3)
         values(0, P, N, 1)
         values(1, 0, P, 2)
-        values(1, P, LATE, 0)
-        project(1, LATE, N, 0)
+        values(1, P, LATE, 3)
+        project(1, LATE, N, 3)
         warm = h_bank[1, LATE][:, N:PASS]
         for turn in range(3):
             nc.tensor.matmul_mx(

from contextlib import ExitStack

import concourse.mybir as mybir
from concourse.masks import make_identity

K, T, S, N, V, W = 512, 4096, 1024, 256, 512, 1024
FLOPS = 2 * S * K * N + 2 * S * K * V + 2 * S * N * V

F32 = mybir.dt.float32
BF16 = mybir.dt.bfloat16
I32 = mybir.dt.int32
U32 = mybir.dt.uint32
U16 = mybir.dt.uint16
U8 = mybir.dt.uint8
FP8X4 = mybir.dt.float8_e4m3fn_x4
ACT = mybir.ActivationFunctionType
ALU = mybir.AluOpType

P = 128
PACK = 4
PASS = P * PACK
GROUPS = S // PASS
RUN = 8
HALF = V // 2
CHUNKS = ((0, 256), (256, 384), (384, 512))
FREE_ROWS = P - 16
TOKEN_ROWS = 2 * GROUPS
TILES = GROUPS * PACK
LATE = N - 64


def tile_picked_yslot_soft_p_kernel(
    tc, x_words, x_scales, e_words, e_scales, mask, wv, inv, offs, slot, out
):
    nc = tc.nc
    with ExitStack() as ctx:
        keep = ctx.enter_context(tc.tile_pool(name="keep", bufs=1))
        psum = ctx.enter_context(tc.psum_pool(name="psum", bufs=1))

        def sb(name, shape, dtype, tag=None):
            return keep.tile(shape, dtype, name=name, tag=tag or name, align_bytes=64)

        def dma_tile(name, shape, dtype):
            return keep.tile(shape, dtype, name=name, align_bytes=256)

        def bank(name, number, shape):
            return psum.tile(shape, F32, name=name, tag="bank%d" % number)

        offs_sb = keep.tile([P, S // 16], U16, name="offs_sb")
        slot_sb = keep.tile([P, V // 16], U16, name="slot_sb")
        xw_all = dma_tile("xw_all", [P, T], I32)
        ew_all = dma_tile("ew_all", [P, W], I32)
        xs_all = dma_tile("xs_all", [P, T], U8)
        es_all = dma_tile("es_all", [P, W], U8)
        wv_raw = dma_tile("wv_raw", [P, PACK, N], F32)
        token_list = dma_tile("token_list", [TOKEN_ROWS, PASS], F32)
        token_rows = sb("token_rows", [P, PACK, P], F32)
        token_cols = sb("token_cols", [P, TOKEN_ROWS, PACK], F32)
        identity = sb("identity", [P, P], F32)

        scales = dma_tile("scales", [P, S + V], U8)
        nc.gpsimd.memset(xs_all[0:FREE_ROWS, :].bitcast(I32), 0)
        nc.vector.memset(es_all[0:FREE_ROWS, :].bitcast(I32), 0)
        nc.vector.memset(scales[:].bitcast(I32), 0)

        nc.sync.dma_start(offs_sb[:], offs)
        nc.sync.dma_start(xs_all[FREE_ROWS:P, :].bitcast(I32), x_scales[0].bitcast(I32))
        nc.scalar.dma_start(es_all[FREE_ROWS:P, :].bitcast(I32), e_scales[0].bitcast(I32))
        nc.sync.dma_start(slot_sb[:], slot)
        nc.sync.dma_start(ew_all[:], e_words[0].rearrange("p n t -> p (n t)").bitcast(I32))
        nc.sync.dma_start(xw_all[:], x_words[0].rearrange("p n t -> p (n t)").bitcast(I32))
        nc.sync.dma_start(wv_raw[:], wv.rearrange("(p j) m -> p j m", j=PACK))
        for row, src in ((0, mask), (GROUPS, inv)):
            nc.scalar.dma_start(token_list[row : row + GROUPS, :], src.rearrange("(g t) o -> g (t o)", g=GROUPS))
        nc.gpsimd.memset(token_rows[:], 0.0)
        make_identity(nc, identity[:])
        nc.scalar.activation(
            token_rows[0:TOKEN_ROWS].rearrange("r j (b i) -> r j b i", i=RUN),
            token_list[:].rearrange("r (b j i) -> r j b i", j=PACK, i=RUN),
            ACT.Copy,
        )
        turned = bank("turned", 7, [P, PACK, P])
        for j in range(PACK):
            nc.tensor.transpose(turned[:, j, :], token_rows[:, j, :], identity[:])
        nc.scalar.activation(token_cols[:], turned[:, :, 0:TOKEN_ROWS].rearrange("p j r -> p r j"), ACT.Copy)

        listed = sb("listed", [P, S + V], U8)
        dealt = dma_tile("dealt", [P, S + V], U8)
        xw = {}
        ew = sb("ew", [P, V], U32)

        nc.vector.tensor_copy(listed[:, 0:S], xs_all[:].indirect(offs_sb[:]))
        nc.vector.tensor_copy(listed[:, S : S + V], es_all[:].indirect(slot_sb[:]))
        nc.vector.tensor_copy(
            dealt[:].bitcast(I32).rearrange("p (g j b w) -> p g j b w", g=GROUPS + 1, j=PACK, w=RUN // 4),
            listed[:].bitcast(I32).rearrange("p (g b j w) -> p g j b w", g=GROUPS + 1, j=PACK, w=RUN // 4),
        )
        for q in (0, 2, 1, 3):
            nc.sync.dma_start(
                scales[32 * q : 32 * q + 4, :].bitcast(I32),
                dealt[FREE_ROWS + 4 * q : FREE_ROWS + 4 * q + 4, :].bitcast(I32),
            )

        def gather_slots():
            nc.vector.tensor_copy(
                ew[:].rearrange("p (j b i) -> p b j i", j=PACK, i=RUN), ew_all[:].bitcast(U32).indirect(slot_sb[:])
            )

        def gather_tokens(g):
            xw[g] = sb("xw%d" % g, [P, PASS], U32)
            nc.vector.tensor_copy(
                xw[g][:].rearrange("p (j b i) -> p b j i", j=PACK, i=RUN),
                xw_all[:].bitcast(U32).indirect(offs_sb[:, g * PASS // 16 : (g + 1) * PASS // 16]),
            )

        wv_bf = sb("wv_bf", [P, N, PACK], BF16)
        wv_w = sb("wv_w", [P, N], U32)

        def weave(copy, woven, rows):
            copy(woven.rearrange("p (c i) j -> p c j i", i=4), rows.rearrange("p j (c i) -> p c j i", i=4))

        def quantize(words, scale_bytes, woven):
            nc.vector.quantize_mx(words.bitcast(FP8X4), scale_bytes, woven.rearrange("p m j -> p (m j)"))

        def token_operand(s):
            g, j = divmod(s, PACK)
            return dict(
                lhsT=xw[g][:, j * P : (j + 1) * P].bitcast(FP8X4), lhsT_scale=scales[:, s * P : (s + 1) * P]
            )

        def mask_of(s):
            g, j = divmod(s, PACK)
            return token_cols[:, g, j : j + 1]

        BATCHES = ((0,), (1, 2), (3, 4, 5), (6, 7))
        neg_max = [sb("neg_max%d" % s, [P, 1], F32) for s in range(TILES)]
        total = [sb("total%d" % u, [P, len(batch)], F32) for u, batch in enumerate(BATCHES)]
        recip = [sb("recip%d" % u, [P, len(batch)], F32) for u, batch in enumerate(BATCHES)]
        factor = {s: sb("factor%d" % s, [P, 1], F32) for s in (4, 5)}
        ex = [sb("ex%d" % s, [P, V], F32) for s in range(TILES)]
        PARTS = (1, 2)
        a_pairs = [sb("a_pairs%d" % g, [P, n, 2, V // n, 2], BF16) for g, n in enumerate(PARTS)]
        h_woven = [sb("h_woven%d" % g, [P, N, PACK], BF16) for g in range(GROUPS)]
        h_words = sb("h_words", [P, GROUPS * N], U32)
        h_scales = sb("h_scales", [P, GROUPS * N], U8)
        h_w = [h_words[:, g * N : (g + 1) * N] for g in range(GROUPS)]
        h_s = [h_scales[:, g * N : (g + 1) * N] for g in range(GROUPS)]
        a_w = [sb("a_w%d" % g, [P, V], U32) for g in range(GROUPS)]
        a_s = [sb("a_s%d" % g, [P, V], U8) for g in range(GROUPS)]
        a_half = {}
        a_chunk = {}

        def column(tiles, s, n=1):
            u = [s in batch for batch in BATCHES].index(True)
            first = s - BATCHES[u][0]
            return tiles[u][:, first : first + n]

        def logits(s, number):
            y = bank("y%d" % s, number, [P, V])
            nc.tensor.matmul_mx(
                y[:], rhs=ew[:].bitcast(FP8X4), rhs_scale=scales[:, S : S + V], start=True, stop=True, **token_operand(s)
            )
            nc.vector.tensor_reduce(neg_max[s][:], y[:], mybir.AxisListType.X, ALU.max, negate=True)
            nc.scalar.activation(
                ex[s][:].rearrange("p (b j i) -> p j b i", j=PACK, i=RUN),
                y[:].rearrange("p (j b i) -> p j b i", j=PACK, i=RUN),
                ACT.Exp,
                bias=neg_max[s][:],
                accum_out=column(total, s),
            )

        h_bank = {}

        def project(g, lo, hi, number):
            h_bank[g, lo] = bank("h%d_%d" % (g, lo), number, [P, PASS])
            for j in range(PACK):
                nc.tensor.matmul_mx(
                    h_bank[g, lo][:, j * (hi - lo) : (j + 1) * (hi - lo)], rhs=wv_w[:, lo:hi].bitcast(FP8X4),
                    rhs_scale=wv_s[:, lo:hi], start=True, stop=True, **token_operand(PACK * g + j)
                )

        def scale_values(g, lo, hi):
            nc.vector.tensor_tensor(
                h_woven[g][:, lo:hi, :].rearrange("p (c i) j -> p c j i", i=2),
                token_cols[:, GROUPS + g, :].unsqueeze(1).unsqueeze(3).to_broadcast([P, (hi - lo) // 2, PACK, 2]),
                h_bank[g, lo][:, 0 : PACK * (hi - lo)].rearrange("p (j c i) -> p c j i", j=PACK, i=2),
                ALU.mult,
            )

        def values(g, lo, hi, number):
            project(g, lo, hi, number)
            scale_values(g, lo, hi)

        def reciprocals(u):
            nc.vector.reciprocal(recip[u][:], total[u][:])

        def rows_of(s):
            g, j = divmod(s, PACK)
            return a_pairs[g][:, :, j // 2, :, j % 2]

        def words_of(g, lo, hi):
            part, first = divmod(lo, V // PARTS[g])
            words = a_pairs[g][:, part].rearrange("p u v e -> p u (v e)").bitcast(U32)
            return words[:, :, first : first + hi - lo]

        def halves_of(s):
            return ex[s][:].rearrange("p (h v) -> p h v", h=PARTS[s // PACK])

        def weights_on(engine, s):
            engine.tensor_scalar(rows_of(s), halves_of(s), column(recip, s), mask_of(s), ALU.mult, ALU.mult)

        def half_weights(s, u):
            nc.vector.tensor_scalar(
                rows_of(s)[:, u], halves_of(s)[:, u], column(recip, s), mask_of(s), ALU.mult, ALU.mult
            )

        def factors(s):
            nc.scalar.activation(factor[s][:], column(recip, s), ACT.Copy, scale=mask_of(s))

        def weights(s):
            nc.scalar.activation(rows_of(s), halves_of(s), ACT.Copy, scale=factor[s][:])

        acc = {}

        def update(g, c, first):
            lo, hi = CHUNKS[c]
            for mh in range(2):
                if first:
                    acc[c, mh] = bank("acc%d_%d" % (c, mh), (4, 5, 6, 7, 2, 1)[2 * c + mh], [P, hi - lo])
                cols = slice(mh * P, (mh + 1) * P)
                nc.tensor.matmul_mx(
                    acc[c, mh][:],
                    lhsT=h_w[g][:, cols].bitcast(FP8X4),
                    lhsT_scale=h_s[g][:, cols],
                    rhs=a_w[g][:, lo:hi].bitcast(FP8X4),
                    rhs_scale=a_s[g][:, lo:hi],
                    start=first,
                    stop=not first,
                )

        def store(chunks, halves, copies):
            lo, hi = CHUNKS[chunks[0]][0], CHUNKS[chunks[-1]][1]
            result = dma_tile("result%d_%d" % (chunks[0], halves[0]), [P, len(halves), hi - lo], F32)
            for c in chunks:
                for e, mh in enumerate(halves):
                    copies[c - chunks[0]][e](result[:, e, CHUNKS[c][0] - lo : CHUNKS[c][1] - lo], acc[c, mh][:])
            rows = out[halves[0] * P : (halves[-1] + 1) * P, lo:hi]
            nc.sync.dma_start(rows.rearrange("(h p) v -> p h v", p=P), result[:])

        def weave_half(u):
            a_half[u] = sb("a_half%d" % u, [P, HALF, PACK], BF16, "ex7" if u else None)
            weave(nc.scalar.copy, a_half[u][:].bitcast(U32), words_of(0, u * HALF, (u + 1) * HALF))

        def quantize_half(u):
            cols = slice(u * HALF, (u + 1) * HALF)
            quantize(a_w[0][:, cols], a_s[0][:, cols], a_half[u][:])

        def weave_chunk(copy, c):
            lo, hi = CHUNKS[c]
            a_chunk[c] = sb("a_chunk%d" % c, [P, hi - lo, PACK], BF16)
            weave(copy, a_chunk[c][:].bitcast(U32), words_of(1, lo, hi))

        def quantize_chunk(c):
            lo, hi = CHUNKS[c]
            quantize(a_w[1][:, lo:hi], a_s[1][:, lo:hi], a_chunk[c][:])

        gather_slots()
        gather_tokens(0)
        gather_tokens(1)
        weave(nc.scalar.copy, wv_bf[:], wv_raw[:])
        logits(0, 0)
        logits(1, 1)
        wv_s = sb("wv_s", [P, N], U8, "neg_max0")
        reciprocals(0)
        quantize(wv_w[:], wv_s[:], wv_bf[:])
        weights_on(nc.gpsimd, 0)
        logits(2, 2)
        logits(3, 3)
        logits(4, 0)
        reciprocals(1)
        weights_on(nc.gpsimd, 1)
        weights_on(nc.gpsimd, 2)
        logits(5, 1)
        logits(6, 2)
        reciprocals(2)
        factors(4)
        factors(5)
        logits(7, 3)
        weights_on(nc.gpsimd, 3)
        values(0, 0, P, 0)
        reciprocals(3)
        values(0, P, N, 1)
        values(1, 0, P, 2)
        values(1, P, LATE, 3)
        project(1, LATE, N, 3)
        warm = h_bank[1, LATE][:, N:PASS]
        for turn in range(3):
            nc.tensor.matmul_mx(
                warm, lhsT=wv_w[:, 0:P].bitcast(FP8X4), lhsT_scale=wv_s[:, 0:P], rhs=wv_w[:].bitcast(FP8X4),
                rhs_scale=wv_s[:], start=True, stop=True,
            )
        weights(4)
        weights(5)
        weave_half(0)
        quantize(h_w[0], h_s[0], h_woven[0][:])
        half_weights(6, 0)
        half_weights(7, 0)
        scale_values(1, LATE, N)
        quantize_half(0)
        update(0, 0, True)
        half_weights(6, 1)
        half_weights(7, 1)
        weave_chunk(nc.scalar.copy, 0)
        weave_half(1)
        weave_chunk(nc.scalar.copy, 1)
        weave_chunk(nc.scalar.copy, 2)
        quantize(h_w[1], h_s[1], h_woven[1][:])
        quantize_chunk(0)
        update(1, 0, False)
        quantize_half(1)
        update(0, 1, True)
        update(0, 2, True)
        quantize_chunk(1)
        update(1, 1, False)
        quantize_chunk(2)
        update(1, 2, False)
        store((0,), (0,), ((nc.scalar.copy,),))
        store((0,), (1,), ((nc.scalar.copy,),))
        store((1, 2), (0, 1), ((nc.scalar.copy, nc.vector.tensor_copy), (nc.scalar.copy, nc.vector.tensor_copy)))
